import numpy as np, ml_dtypes
CORES = [66,74,82,90,194,202,210,218]
N = 8
BF = ml_dtypes.bfloat16
def gentries(a):
    return np.ascontiguousarray(a.reshape(8, 16, -1).transpose(0, 2, 1)).reshape(8, -1)
def gtable(e):
    e = np.asarray(e); return np.ascontiguousarray(e.reshape(8, -1, 16).transpose(0, 2, 1)).reshape(128, -1).astype(np.int32)
R, H, LO, UP, SW = 224, 32, 3, 6, 3
S, M, T = LO + 1 + UP, N * R, R + (N - 1) * H
def byrank(v):
    return np.ascontiguousarray(v.reshape(8, -1, R, N).transpose(3, 0, 1, 2)).reshape(N, 8, -1)
def ships(rng, rows):
    return np.argsort(rng.random((N, 8, N - 1, rows)), axis=-1)[..., :H]
def users(rng, low):
    u = np.full((8, M), -1, np.int64)
    for g in range(8):
        for t in rng.permutation(LO):
            o = rng.permutation(M); l = low[g, t, o]; ok = l >= 0; u[g, l[ok]] = o[ok]
    return u
def grow(rng, ship, far, drop=0.05, sweep=False):
    G = np.arange(8)[:, None]; i = np.arange(M); q = i % N; n = i // N; K = (N - 1) * H
    low = np.empty((8, LO, M), np.int64); spot = np.empty((8, LO, M), np.int64); up = np.empty((8, UP, M), np.int64)
    for t in range(LO):
        e = rng.integers(0, K, (8, M))
        if sweep: e = np.where(n >= R // 2, ((n - R // 2) * LO + t) % K, e)
        b = e // H; p = b + (b >= q); k = ship[p, G, q - (q > p), e % H] * N + p
        take = (rng.random((8, M)) < far) & (k < i); own = (rng.random((8, M)) * n).astype(np.int64)
        c = np.where(take, k, own * N + q); none = (~take & (n == 0)) | (rng.random((8, M)) < drop)
        for s in range(t): none |= c == low[:, s]
        low[:, t] = np.where(none, -1 - t, c); spot[:, t] = np.where(none, rng.integers(0, T, (8, M)), np.where(take, R + e, own))
    u = users(rng, low); cand = []
    for x in (u, users(rng, low)):
        v = np.maximum(x, 0); l = low[G, rng.integers(0, LO, (8, M)), v]
        cand += [x, np.where((x >= 0) & (l > i), l, -1), np.where(x >= 0, u[G, v], -1)]
    cand = np.stack(cand); turn = rng.integers(0, UP, (8, M))
    for w in range(UP):
        c = cand[(w + turn) % UP, G, i]; other = i + 1 + (rng.random((8, M)) * (M - 1 - i)).astype(np.int64)
        good = (c > i) & (rng.random((8, M)) < 0.85)
        for s in range(w): good &= c != up[:, s]
        c = np.where(good, c, other); none = (c >= M) | (rng.random((8, M)) < 0.04)
        for s in range(w): none |= c == up[:, s]
        up[:, w] = np.where(none, M + w, c)
    return low, spot, up
def fill(rng, ship, low, spot, up):
    c = np.concatenate([low, np.broadcast_to(np.arange(M), (8, 1, M)), up], 1); real = byrank((c >= 0) & (c < M)).reshape(N, 8, 1, S, R)
    v = (0.03 + 0.09 * rng.random((N, 8, 16, S, R))) * (2 * rng.integers(0, 2, (N, 8, 16, S, R)) - 1)
    v = np.where(real, v, 0.0); v[:, :, :, LO] = 0.75 + 0.75 * rng.random((N, 8, 16, R))
    return {"val": v.reshape(N, 128, S * R).astype(BF), "col": byrank(c).astype(np.int32), "spot": np.stack([gtable(x) for x in byrank(spot)]), "ship": np.stack([gtable(x.reshape(8, -1)) for x in ship])}
def setup_inputs(rng):
    ship = ships(rng, R); return fill(rng, ship, *grow(rng, ship, 0.8))
def setup_inputs_halo(rng):
    ship = ships(rng, R // 2); return fill(rng, ship, *grow(rng, ship, 1.0, 0.0, True))
def setup_inputs_hub(rng):
    ship = rng.integers(0, 3, (N, 8, N - 1, H)); return fill(rng, ship, *grow(rng, ship, 0.95))
def setup_inputs_thin(rng):
    ship = ships(rng, R); low, spot, up = grow(rng, ship, 0.8)
    gone = rng.random((8, 1, M)) < rng.permutation(np.array([1.0, 1.0, 0.95, 0.8, 0.5, 0.5, 0.1, 0.0]))[:, None, None]
    gone = gone | (np.arange(M) % N == rng.integers(0, N))
    low = np.where(gone, -1 - np.arange(LO)[:, None], low); up = np.where(gone, M + np.arange(UP)[:, None], up)
    return fill(rng, ship, low, spot, up)
def setup_inputs_band(rng):
    ship = ships(rng, R); low, spot, up = grow(rng, ship, 0.8); n = np.arange(M) // N; q = np.arange(M) % N
    for g in range(6):
        for t in range(LO):
            b = n - (t + 1) * (g + 1); low[g, t] = np.where(b >= 0, b * N + q, -1 - t); spot[g, t] = np.where(b >= 0, b, 0)
        for w in range(UP):
            b = n + (w + 1) * (g + 1); up[g, w] = np.where(b < R, b * N + q, M + w)
    d = fill(rng, ship, low, spot, up); v = np.sign(d["val"].astype(np.float32)).reshape(N, 8, 16, S, R) * (0.125 - rng.integers(0, 4, (N, 8, 16, S, R)) * 2.0 ** -11)
    v[:, :, :, LO] = rng.choice(np.array([0.75, 0.75390625, 1.4921875, 1.5]), (N, 8, 16, R)); d["val"] = v.reshape(N, 128, S * R).astype(np.float32).astype(BF); return d
def setup_inputs_spread(rng):
    d = setup_inputs(rng); k = np.exp2(rng.integers(-6, 1, (N, 8, 1, S, R))) * (rng.random((N, 8, 1, S, R)) > 0.0625); k[:, :, :, LO] = 1
    d["val"] = (d["val"].astype(np.float32).reshape(N, 8, 16, S, R) * k).reshape(N, 128, S * R).astype(BF); return d
def check_inputs(d):
    bad = []; i = np.arange(R)[None] * N + np.arange(N)[:, None]; row = i[:, None, None]
    c = d["col"].astype(np.int64).reshape(N, 8, S, R); lo, up = c[:, :, :LO], c[:, :, LO + 1:]
    elo = lo == -1 - np.arange(LO)[:, None]; eup = up == M + np.arange(UP)[:, None]
    if not (c[:, :, LO] == i[:, None]).all(): bad.append("the diagonal's column is the row's number")
    if not (elo | ((lo >= 0) & (lo < row))).all(): bad.append("lower columns are below the row's number, or the slot is empty")
    if not (eup | ((up > row) & (up < M))).all(): bad.append("upper columns are above the row's number, or the slot is empty")
    s = np.sort(c, axis=2)
    if (s[:, :, 1:] == s[:, :, :-1]).any(): bad.append("the columns of a row differ")
    v = d["val"].astype(np.float32).reshape(N, 8, 16, S, R); e = np.concatenate([elo, np.zeros((N, 8, 1, R), bool), eup], 2)[:, :, None]
    if not ((v[:, :, :, LO] >= 0.75) & (v[:, :, :, LO] <= 1.5)).all(): bad.append("diagonals lie from 0.75 to 1.5")
    if not (np.abs(np.delete(v, LO, 3)) <= 0.125).all(): bad.append("other values are at most 0.125 in size")
    if not ((v == 0) | ~e).all(): bad.append("empty slots have the value 0")
    sh = np.stack([gentries(x) for x in d["ship"]]).astype(np.int64).reshape(N, 8, N - 1, H); sp = np.stack([gentries(x) for x in d["spot"]]).astype(np.int64)
    if not ((sh >= 0) & (sh < R)).all(): bad.append("ship names local rows")
    if not ((sp >= 0) & (sp < T)).all(): bad.append("spot holds places")
    for q in range(N):
        tab = np.concatenate([np.broadcast_to(i[q], (8, R))] + [sh[p][:, q - (q > p)] * N + p for p in range(N) if p != q], 1)
        k = np.take_along_axis(tab, np.clip(sp[q], 0, T - 1), 1).reshape(8, LO, R)
        if not ((k == lo[q]) | elo[q]).all(): bad.append("the row at a lower slot's place is its column"); break
    return bad
def reference(val, col, spot, ship):
    c = col.astype(np.int64).reshape(N, 8, S, R).transpose(1, 2, 3, 0).reshape(8, S, M)
    a = val.astype(np.float64).reshape(N, 8, 16, S, R).transpose(1, 2, 3, 4, 0).reshape(8, 16, S, M)
    y = np.empty((8, 16, S, M)); z = np.empty((8, 16, M))
    for g in range(8):
        k = np.maximum(c[g, :LO], 0)
        at = np.full((S, LO, M), UP * M, np.int64)
        for w in range(UP): at = np.where(c[g, LO + 1 + w][k][None] == c[g][:, None], w * M + k[None], at)
        x = a[g]; r = np.ones((16, M))
        for sweep in range(SW):
            u = np.concatenate([x[:, LO + 1:].reshape(16, UP * M), np.zeros((16, 1))], 1); d = np.array(a[g])
            for t in range(LO): d -= x[:, t][:, None] * u[:, at[:, t]]
            for t in range(LO): d[:, t] *= r[:, k[t]]
            r = r * (2 - x[:, LO] * r); x = d
        y[g] = x; z[g] = r
    y = y.reshape(8, 16, S, R, N).transpose(4, 0, 1, 2, 3).reshape(N, 128, S * R); z = z.reshape(8, 16, R, N).transpose(3, 0, 1, 2).reshape(N, 128, R)
    return {"y": y.astype(np.float32), "inv": z.astype(np.float32)}

@@ -1,0 +1,453 @@
+from concourse.bass import DstId, RemoteDMATransfer
+from concourse.mybir import AluOpType as Op, ActivationFunctionType as Act
+
+R, H, NB = 224, 32, 7
+BLK = 6 * H
+HALO = 16
+OWN = HALO + NB * BLK
+WIN = OWN + 6 * R
+LIFT = 1400
+F32, BF, F16, I32, U16 = "float32", "bfloat16", "float16", "int32", "uint16"
+
+SCRATCH = {
+    "shipI": ("sbuf", [128, 14], I32), "shipU": ("sbuf", [128, 14], U16),
+    "spotI": ("sbuf", [128, 42], I32), "spotU": ("sbuf", [128, 42], U16), "spotF": ("sbuf", [128, 126], F32),
+    "lg": ("sbuf", [128, 126], F32), "lm": ("sbuf", [128, 126], F32), "lc": ("sbuf", [128, 126], F32),
+    "strR": ("sbuf", [128, 126], F32), "baseR": ("sbuf", [128, 126], F32), "jt": ("sbuf", [128, 378], F32),
+    "lr": ("sbuf", [128, 84], F32), "offR": ("sbuf", [128, 84], U16), "off": ("sbuf", [128, 378], U16),
+    "colI": ("sbuf", [128, R], I32), "colF": ("sbuf", [128, 2 * R], F32), "sndC": ("sbuf", [128, R], F32),
+    "colT": ("sbuf", [128, 14, 16], F32), "rep": ("sbuf", [128, 14, 10, 6], F32), "rep3": ("sbuf", [128, 42, 9, 6], F32),
+    "cug": ("sbuf", [128, 3 * R], F32), "eq": ("sbuf", [128, 9 * 252], F16),
+    "ioJ": ("sbuf", [128, 128], F32), "ioK": ("sbuf", [128, 128], F32),
+    "idB": ("sbuf", [128, 128], BF), "idN": ("sbuf", [128, 128], F32),
+    "W0": ("sbuf", [128, 512], F16), "W": ("sbuf", [128, 6 * 512], F16),
+    "lowd": ("sbuf", [128, 4 * R], BF), "A": ("sbuf", [128, WIN], BF),
+    "U1": ("sbuf", [128, WIN], F32), "U2": ("sbuf", [128, WIN], F32),
+    "sndA": ("sbuf", [128, NB * BLK], BF), "snd1": ("sbuf", [128, NB * BLK], F32), "snd2": ("sbuf", [128, NB * BLK], F32),
+    "relA": ("sbuf", [128, BLK], BF), "rel1": ("sbuf", [128, BLK], F32), "rel2": ("sbuf", [128, BLK], F32),
+    "Rw": ("sbuf", [128, 4 * R], F32), "sndR": ("sbuf", [128, 2 * R], F32),
+    "G": ("sbuf", [128, 9 * 2 * R], F32), "P2": ("sbuf", [128, 9 * R], F32),
+    "x2": ("sbuf", [128, 2 * R], F32), "rg": ("sbuf", [128, 6 * R], F32),
+    "rq": ("sbuf", [128, 2 * R], F32), "rr": ("sbuf", [128, 2 * R], F32), "r3": ("sbuf", [128, R], F32),
+    "Y": ("sbuf", [128, 10 * R], F32),
+    "cut": ("psum", [128, 64, 16], F32),
+    "X0": ("psum", [128, 512], F32), "X1": ("psum", [128, 512], F32), "D": ("psum", [128, 512], F32),
+    "B0": ("psum", [128, 512], F32), "B1": ("psum", [128, 512], F32), "B2": ("psum", [128, 512], F32),
+}
+SEMAPHORES = ["cv", "cs", "cp", "cg", "lship", "lspot", "lcol", "lup", "llow", "st",
+              "arC", "arA", "ar1", "ar2", "arR", "hA", "h1", "h2", "sent"]
+ROUNDS = (("A", "sndA", "relA", "A"), ("1", "snd1", "rel1", "U1"), ("2", "snd2", "rel2", "U2"))
+
+
+def bits(engines):
+    m = 0
+    for e in engines:
+        m |= 1 << e
+    return m
+
+
+def routes(T, topo):
+    cores, n, plan = T.cores, len(T.cores), []
+    for p, c in enumerate(cores):
+        order = [(p + k) % n for k in range(1, n)]
+        mate = [q for q in order if topo.mates(c, cores[q])]
+        plane = [q for q in order if topo.same_plane(c, cores[q])]
+        far = [q for q in order if q not in mate and q not in plane]
+        free = [h for h in topo.cores_of(c) if topo.die(h) != topo.die(c)]
+        relay = []
+        for q in far[1:] + plane[:1]:
+            h = [h for h in free if topo.may_write(h, cores[q])][0]
+            free.remove(h)
+            relay.append((h, q))
+        plan.append((mate + far[:1] + plane[1:], relay))
+    return plan
+
+
+def landing(buf, lo, width, p, q):
+    b = p if p < q else p - 1
+    return buf[:, lo + b * width:lo + (b + 1) * width]
+
+
+def helper_program(g, core, T, topo, p, i, q):
+    dst = T.cores[q]
+    rid, pid = topo.addr(dst, core)
+    n = len(topo.engines(core, dst))
+    got = n if i == 2 else n // 2
+    for name, _, rel, win in ROUNDS:
+        g.wait_ge(T.sem["h" + name], got)
+        g.remote_dma(landing(T[win], HALO, BLK, p, q), T[rel][:], T.sem["ar" + name], T.sem.sent, pid, rid, topo.mask(core, dst))
+    g.wait_ge(T.sem.sent, n * len(ROUNDS))
+
+
+def rank_program(g, core, T, topo):
+    rank = T.rank_of(core)
+    plan = routes(T, topo)
+    if rank is None:
+        for p, (_, relay) in enumerate(plan):
+            for i, (h, q) in enumerate(relay):
+                if h == core:
+                    helper_program(g, core, T, topo, p, i, q)
+        return
+    cores = T.cores
+    direct, relay = plan[rank]
+    V, S, P, Q = g.vector, g.scalar, g.tensor, g.sync
+    eng = {"v": V, "s": S, "p": P, "q": Q, "g": g}
+    count = {"cv": 0, "cs": 0, "cp": 0, "cg": 0}
+    seen = {k: {} for k in eng}
+    wr, rd = {}, {}
+
+    def need(q, tok):
+        if seen[q].get(tok[0], 0) < tok[1]:
+            seen[q][tok[0]] = tok[1]
+            eng[q].wait_ge(T.sem[tok[0]], tok[1])
+
+    def order(q, reads, writes, chain=False):
+        toks = {}
+        for r in reads:
+            if r in wr:
+                toks[wr[r][0]] = max(toks.get(wr[r][0], 0), wr[r][1])
+        for w in writes:
+            for t in rd.get(w, []) + ([wr[w]] if w in wr and not chain else []):
+                toks[t[0]] = max(toks.get(t[0], 0), t[1])
+        for t in toks.items():
+            need(q, t)
+
+    def mark(tok, reads, writes):
+        for r in reads:
+            rd.setdefault(r, []).append(tok)
+        for w in writes:
+            wr[w] = tok
+            rd[w] = []
+
+    def op(q, reads, writes, call, chain=False):
+        order(q, reads, writes, chain)
+        sem = "c" + q
+        count[sem] += 1
+        call().then_inc(T.sem[sem], 1)
+        mark((sem, count[sem]), reads, writes)
+
+    def dma(q, sem, total, out, in_, reads, writes):
+        order(q, reads, writes)
+        eng[q].dma_start(out, in_).then_inc(T.sem[sem], 16)
+        mark((sem, total), reads, writes)
+
+    off_chip = topo.engines(core, cores[direct[0]])
+    on_chip = [e for e in topo.engines(core, relay[0][0]) if e not in off_chip]
+    ne = len(off_chip)
+    sent = [0]
+
+    def piece(snd, width, q):
+        b = q if q < rank else q - 1
+        return T[snd][:, b * width:(b + 1) * width]
+
+    def dst_id(c):
+        rid, pid = topo.addr(c, core)
+        return DstId(rid=rid, pnc=pid)
+
+    def exchange(k, reads):
+        name, snd, rel, win = ROUNDS[k]
+        order("g", reads, [])
+        d, h = ne // len(direct), len(on_chip) // 2
+        tr = [RemoteDMATransfer(dst_ids=[dst_id(cores[q])], dma_engine_mask=bits(off_chip[i * d:(i + 1) * d]),
+                                remote_sem=T.sem["ar" + name], src=piece(snd, BLK, q), dst=landing(T[win], HALO, BLK, rank, q))
+              for i, q in enumerate(direct)]
+        tr += [RemoteDMATransfer(dst_ids=[dst_id(c)], dma_engine_mask=bits(on_chip[i * h:(i + 1) * h]),
+                                 remote_sem=T.sem["h" + name], src=piece(snd, BLK, q), dst=T[rel][:])
+               for i, (c, q) in enumerate(relay[:2])]
+        g.remote_dma_fused(tr, local_sem=T.sem.sent)
+        c, q = relay[2]
+        rid, pid = topo.addr(c, core)
+        g.remote_dma(T[rel][:], piece(snd, BLK, q), T.sem["h" + name], T.sem.sent, pid, rid, bits(on_chip))
+        sent[0] += ne + 2 * len(on_chip)
+        wr["halo" + name] = ("ar" + name, ne + ne * len(relay))
+
+    def small(name, snd, buf, lo, width, reads):
+        order("g", reads, [])
+        to = direct + [q for _, q in relay]
+        g.remote_dma_fused([RemoteDMATransfer(dst_ids=[dst_id(cores[q])], dma_engine_mask=bits(off_chip[i:i + 1]),
+                                              remote_sem=T.sem["ar" + name], src=piece(snd, width, q),
+                                              dst=landing(T[buf], lo, width, rank, q)) for i, q in enumerate(to)],
+                           local_sem=T.sem.sent)
+        sent[0] += len(to)
+        wr["halo" + name] = ("ar" + name, len(to))
+
+    op("v", [], ["colI"], lambda: V.memset(T.colI[:], 0))
+    dma("q", "lship", 16, T.shipI[:], T.ship[:], [], ["shipI"])
+    dma("s", "lspot", 16, T.spotI[:], T.spot[:], [], ["spotI"])
+    order("q", ["colI"], [])
+    order("s", ["colI"], [])
+    for k in range(8):
+        dma("qs"[k % 2], "lcol", 128, T.colI[16 * k:16 * k + 10, :], T.col[k, :], [], [])
+    wr["colI"] = ("lcol", 128)
+    dma("q", "lup", 16, T.A[:, OWN:WIN], T.val[:, 4 * R:10 * R], [], ["Aup"])
+    dma("s", "llow", 16, T.lowd[:], T.val[:, 0:4 * R], [], ["lowd"])
+    op("g", [], ["ioJ"], lambda: g.iota(T.ioJ[:], [[-32, 4], [1000, 2], [-1, 16]], 0, 1, allow_small_or_imprecise_dtypes=True))
+    op("g", [], ["ioK"], lambda: g.iota(T.ioK[:], [[-1, 128]], 0, 1, allow_small_or_imprecise_dtypes=True))
+    for win in ("A", "U1", "U2"):
+        op("v", [], [win + "z"], lambda: V.memset(T[win][:, 0:HALO], 0.0))
+    for h in range(2):
+        for e in range(2):
+            lo = (2 * h + e) * 128
+            op("v", ["ioJ"], ["W0"], lambda: V.tensor_scalar(T.W0[:, lo:lo + 128], T.ioJ[:], float(16 * h + 1000 * e), None, Op.is_equal), True)
+
+    def weigh(w):
+        op("v", ["W0"], ["W"], lambda: V.tensor_scalar(T.W[:, 512 * w:512 * w + 512], T.W0[:], float(LIFT + w + 1), None, Op.mult), True)
+
+    weigh(0)
+    weigh(1)
+
+    op("v", ["shipI"], ["shipU"], lambda: V.tensor_copy(T.shipU[:], T.shipI[:]))
+    op("v", ["colI", "shipU"], ["sndC"], lambda: V.tensor_copy(T.sndC[:], T.colI[:, 0:R].indirect(T.shipU[:, 0:14])))
+    small("C", "sndC", "colF", R, H, ["sndC"])
+
+    op("v", ["colI"], ["colF"], lambda: V.tensor_copy(T.colF[:, 0:R], T.colI[:]))
+    op("v", ["spotI"], ["spotU"], lambda: V.tensor_copy(T.spotU[:], T.spotI[:]))
+    for v in range(3):
+        op("v", ["spotI"], ["spotF"], lambda: V.tensor_copy(T.spotF[:, 42 * v:42 * v + 42], T.spotI[:]), True)
+    op("v", ["colF"], ["colT"], lambda: V.transpose(T.colT[:], T.colF[:, 0:R]))
+    op("v", ["spotF"], ["lg"], lambda: V.tensor_scalar(T.lg[:], T.spotF[:], float(R), None, Op.is_ge))
+    for w in range(6):
+        op("s", ["colT"], ["rep"], lambda: S.activation(T.rep[:, :, :, w], T.colT[:, :, 0:10], Act.Copy), True)
+
+    def pick(q, src, out, reads, res):
+        src = src.indirect(T.shipU[:, 0:14])
+        if q == "v":
+            op("v", reads + ["shipU"], [res], lambda: V.tensor_copy(out, src))
+        else:
+            op("s", reads + ["shipU"], [res], lambda: S.activation(out, src, Act.Copy))
+
+    def ship(q, win, snd, c, reads):
+        pick(q, T[win][:, OWN + c * R:OWN + (c + 1) * R], T[snd][:, c:NB * BLK:6], reads, snd + str(c))
+
+    for c in range(3):
+        ship("v", "A", "sndA", c, ["Aup"])
+    for c in range(3, 6):
+        ship("s", "A", "sndA", c, ["Aup"])
+    exchange(0, ["sndA%d" % c for c in range(6)])
+    own0, halo0 = OWN - R - LIFT * R, HALO - 1 - 6 * R - LIFT
+    op("v", ["lg"], ["lm"], lambda: V.tensor_scalar(T.lm[:], T.lg[:], 5.0, 1.0, Op.mult, Op.add))
+    op("v", ["lg"], ["strR"], lambda: V.tensor_scalar(T.strR[:], T.lg[:], float(1 - R), float(R), Op.mult, Op.add))
+    op("v", ["lg"], ["lc"], lambda: V.tensor_scalar(T.lc[:], T.lg[:], float(halo0 - own0), float(own0), Op.mult, Op.add))
+    op("v", ["lm", "spotF"], ["lm"], lambda: V.tensor_tensor(T.lm[:], T.lm[:], T.spotF[:], Op.mult))
+    weigh(2)
+    op("v", ["lm", "lc"], ["baseR"], lambda: V.tensor_tensor(T.baseR[:], T.lm[:], T.lc[:], Op.add))
+    for t, v0, v1, s0 in ((0, 0, 9, 1), (1, 0, 1, 0), (1, 1, 9, 2), (2, 0, 2, 0), (2, 2, 9, 3)):
+        op("s", ["rep"], ["rep3"], lambda: S.activation(T.rep3[:, 14 * t:14 * t + 14, v0:v1, :], T.rep[:, :, s0:s0 + v1 - v0, :], Act.Copy), True)
+    for w in range(3, 6):
+        weigh(w)
+    op("v", ["ioK"], ["idB"], lambda: V.tensor_scalar(T.idB[:], T.ioK[:], 0.0, None, Op.is_equal))
+    op("v", ["ioK"], ["idN"], lambda: V.tensor_scalar(T.idN[:], T.ioK[:], 0.0, -1.0, Op.is_equal, Op.mult))
+    op("p", ["lowd", "idB"], ["X0"], lambda: P.matmul(T.X0[:, 0:2 * R], T.idB[:], T.lowd[:, 0:2 * R], True, True))
+
+    op("s", ["colF", "haloC", "spotU"], ["cug1"], lambda: S.activation(T.cug[:, R:3 * R], T.colF[:, 0:2 * R].indirect(T.spotU[:, 14:42]), Act.Copy))
+    op("v", ["colF", "haloC", "spotU"], ["cug0"], lambda: V.tensor_copy(T.cug[:, 0:R], T.colF[:, 0:2 * R].indirect(T.spotU[:, 0:14])))
+    op("v", ["cug0"], ["cut0"], lambda: V.transpose(T.cut[:, 0:14, :], T.cug[:, 0:R]))
+    op("v", ["cug1"], ["cut1"], lambda: V.transpose(T.cut[:, 14:42, :], T.cug[:, R:3 * R]))
+    diag = T.lowd[:, 3 * R:4 * R]
+    op("s", ["lowd"], ["r1"], lambda: S.activation(T.Rw[:, 0:R], diag, Act.Identity, bias=2.0, scale=-1.0))
+    op("s", ["lowd"], ["rq0"], lambda: S.activation(T.rq[:, 0:R], diag, Act.Square, bias=2.0, scale=-1.0))
+    op("s", ["lowd"], ["rr0"], lambda: S.activation(T.rr[:, 0:R], diag, Act.Identity, bias=4.0, scale=-2.0))
+    pick("s", T.Rw[:, 0:R], T.sndR[:, 0:2 * R:2], ["r1"], "sndR0")
+
+    def compare(v):
+        op("v", ["cut0", "cut1", "rep3"], ["eq%d" % v],
+           lambda: V.tensor_tensor(T.eq[:, 252 * v:252 * v + 252], T.cut[:, 0:42, 4:10], T.rep3[:, :, v, :], Op.is_equal))
+
+    def fold(v0, bank):
+        first = True
+        for h in range(2):
+            for i in range(12):
+                w, e = i // 2, i % 2
+                lo = 512 * w + (2 * h + e) * 128
+                op("p", ["eq%d" % v for v in range(v0, v0 + 3)] + ["W"], [bank],
+                   lambda: P.matmul(T[bank][:, h:126:2], T.W[:, lo:lo + 128],
+                                    T.eq[:, 252 * v0 + 6 * e + w:252 * v0 + 756:12], i == 0, i == 11), not first)
+                first = False
+
+    def place(v0, bank, step):
+        a = 42 * v0
+        if step == 0:
+            op("v", [bank, "strR"], [bank], lambda: V.tensor_tensor(T[bank][:, 0:126], T[bank][:, 0:126], T.strR[:], Op.mult))
+        elif step == 1:
+            op("v", [bank, "baseR"], ["jt%d" % v0], lambda: V.tensor_tensor(T.jt[:, a:a + 126], T[bank][:, 0:126], T.baseR[:], Op.add))
+        else:
+            op("v", ["jt%d" % v0], ["off%d" % v0], lambda: V.tensor_copy(T.off[:, a:a + 126], T.jt[:, a:a + 126]))
+
+    for v in (3, 4, 5):
+        compare(v)
+    fold(3, "X1")
+    compare(6)
+    compare(7)
+    place(3, "X1", 0)
+    compare(8)
+    place(3, "X1", 1)
+    fold(6, "D")
+    place(3, "X1", 2)
+
+    def sweep(k):
+        win = ("A", "U1", "U2")[k]
+        new = ("U1", "U2", None)[k]
+        snd = ("snd1", "snd2", None)[k]
+        whole = [win + "z", "halo" + "A12"[k]] + (["Aup"] if k == 0 else [win + "u%d" % i for i in range(3)])
+        xo, xn = ("X0", "X1", "X0")[k], ("X1", "X0", "X1")[k]
+        dg = "B2" if k == 2 else "B0"
+        x2 = T.lowd[:, 2 * R:3 * R] if k == 0 else T.x2[:, (k - 1) * R:k * R]
+        x2n = "lowd" if k == 0 else "x2%d" % (k - 1)
+        rg = (k - 1) * 3 * R
+
+        def offs(v):
+            return "off%d" % (v // 3 * 3)
+
+        def G(v):
+            op("s", whole + [offs(v)], ["G%d" % v], lambda: S.activation(
+                T.G[:, 2 * R * v:2 * R * (v + 1)], T[win][:, 0:WIN].indirect(T.off[:, 42 * v:42 * v + 28]), Act.Copy))
+
+        def F(v):
+            op("v", whole + [offs(v), x2n], ["P%d" % v], lambda: V.tensor_tensor(
+                T.P2[:, R * v:R * (v + 1)], T[win][:, 0:WIN].indirect(T.off[:, 42 * v + 28:42 * v + 42]), x2, Op.mult))
+
+        def init(bank, src, n, res):
+            op("p", [res, "idB"], [bank], lambda: P.matmul(T[bank][:, 0:n], T.idB[:], src, True, False))
+
+        def sub(bank, lo, src, res, stop):
+            op("p", [res, "idN"], [bank], lambda: P.matmul(T[bank][:, lo:lo + R], T.idN[:], src, False, stop), True)
+
+        def g_part(v, t):
+            return T.G[:, (2 * v + t) * R:(2 * v + t + 1) * R]
+
+        def M(v):
+            gv = T.G[:, 2 * R * v:2 * R * (v + 1)]
+            res = "G%d" % v
+            op("v", [res, xo], [res], lambda: V.tensor_tensor(gv, gv, T[xo][:, 0:2 * R], Op.mult))
+            if v >= 3:
+                i, j = (v - 3) // 2, (v - 3) % 2
+                sub("B%d" % i, j * R, g_part(v, 0), res, False)
+                sub("B%d" % i, j * R, g_part(v, 1), res, j == 1)
+            elif v == 0:
+                sub(xn, R, g_part(0, 0), res, False)
+                sub(xn, 0, g_part(0, 1), res, True)
+            elif v == 1:
+                sub("D", 0, g_part(1, 0), res, False)
+                sub("D", 0, g_part(1, 1), res, True)
+            else:
+                sub(dg, 0, g_part(2, 0), res, False)
+                sub(dg, 0, g_part(2, 1), res, True)
+
+        def store(lo, hi, res):
+            dma("q", "st", 0, T.y[:, lo:hi], T.Y[:, lo:hi], res, [])
+            stores[0] += 16
+
+        def init_up(i):
+            init("B%d" % i, T.A[:, OWN + 2 * i * R:OWN + (2 * i + 2) * R], 2 * R, "Aup")
+
+        def fin(i):
+            v = 3 + 2 * i
+            out = T[new][:, OWN + 2 * i * R:OWN + (2 * i + 2) * R] if new else T.Y[:, (4 + 2 * i) * R:(6 + 2 * i) * R]
+            res = (new or "Y") + "u%d" % i
+            op("v", ["B%d" % i, "P%d" % v, "P%d" % (v + 1)], [res],
+               lambda: V.tensor_tensor(out, T["B%d" % i][:, 0:2 * R], T.P2[:, v * R:(v + 2) * R], Op.subtract))
+            if not new:
+                store((4 + 2 * i) * R, (6 + 2 * i) * R, [res])
+
+        def low_init():
+            init(xn, T.lowd[:, 0:2 * R], 2 * R, "lowd")
+            init("D", T.lowd[:, 2 * R:3 * R], R, "lowd")
+            init(dg, diag, R, "lowd")
+
+        def FL(v):
+            F(v)
+            if v < 2:
+                sub(xn, v * R, T.P2[:, v * R:(v + 1) * R], "P%d" % v, False)
+            elif k < 2:
+                sub(dg, 0, T.P2[:, 2 * R:3 * R], "P2", False)
+
+        def fin2():
+            out, res = (T.x2[:, k * R:(k + 1) * R], "x2%d" % k) if k < 2 else (T.Y[:, 2 * R:3 * R], "Yl2")
+            if k == 0:
+                op("v", ["D"], [res], lambda: V.tensor_copy(out, T.D[:, 0:R]))
+            else:
+                op("v", ["D", "rg%d" % k], [res], lambda: V.tensor_tensor(out, T.D[:, 0:R], T.rg[:, rg + 2 * R:rg + 3 * R], Op.mult))
+
+        def fin01():
+            if k == 0:
+                return
+            out, res = (T[xn][:, 0:2 * R], xn) if k == 1 else (T.Y[:, 0:2 * R], "Yl0")
+            op("v", [xn, "rg%d" % k], [res], lambda: V.tensor_tensor(out, T[xn][:, 0:2 * R], T.rg[:, rg:rg + 2 * R], Op.mult))
+
+        def newton(step):
+            out, res = (T.Rw[:, R:2 * R], "r2") if k == 0 else (T.r3[:], "r3")
+            if step == 0:
+                op("v", [dg, "rq%d" % k], [dg], lambda: V.tensor_tensor(T[dg][:, 0:R], T[dg][:, 0:R], T.rq[:, k * R:(k + 1) * R], Op.mult))
+            else:
+                op("v", [dg, "rr%d" % k], [res], lambda: V.tensor_tensor(out, T.rr[:, k * R:(k + 1) * R], T[dg][:, 0:R], Op.subtract))
+
+        def r_of_lower(j):
+            op("s", ["r1", "r2", "haloR", "offR"], ["rg%d" % (j + 1)], lambda: S.activation(
+                T.rg[:, 3 * R * j:3 * R * (j + 1)], T.Rw[:, 0:4 * R].indirect(T.offR[:, 42 * j:42 * j + 42]), Act.Copy))
+
+        if k < 2:
+            for i in range(3):
+                init_up(i)
+            G(3); G(4); G(5)
+            if k == 0:
+                place(6, "D", 0)
+            F(3)
+            if k == 0:
+                place(6, "D", 1)
+            F(4)
+            if k == 0:
+                place(6, "D", 2)
+            G(6); G(7); G(8)
+            M(3); M(4); F(5); M(5); fin(0); M(6); F(6); M(7)
+            ship("s", new, snd, 0, [new + "u0"]); ship("s", new, snd, 1, [new + "u0"])
+            fin(1); M(8); F(7); F(8)
+            ship("s", new, snd, 2, [new + "u1"]); ship("s", new, snd, 3, [new + "u1"])
+            if k == 1:
+                G(1)
+            fin(2)
+            ship("s", new, snd, 4, [new + "u2"]); ship("v", new, snd, 5, [new + "u2"])
+            exchange(k + 1, [snd + str(c) for c in range(6)])
+            if k == 0:
+                compare(0); compare(1); compare(2)
+                fold(0, "X1")
+                op("v", ["lg"], ["lr0"], lambda: V.tensor_scalar(T.lr[:, 0:42], T.lg[:, 0:42], 1.0, None, Op.add))
+                place(0, "X1", 0)
+                op("v", ["lr0", "spotF"], ["lr0"], lambda: V.tensor_tensor(T.lr[:, 0:42], T.lr[:, 0:42], T.spotF[:, 0:42], Op.mult))
+                place(0, "X1", 1)
+                op("v", ["lr0", "strR"], ["lr1"], lambda: V.tensor_tensor(T.lr[:, 42:84], T.lr[:, 0:42], T.strR[:, 0:42], Op.add))
+                place(0, "X1", 2)
+                op("v", ["lr0", "lr1"], ["offR"], lambda: V.tensor_copy(T.offR[:], T.lr[:]))
+                G(1)
+            low_init()
+            G(0); G(2)
+            if k == 1:
+                r_of_lower(0); r_of_lower(1)
+            FL(0); FL(1); M(1); M(0); FL(2); M(2); fin2(); fin01(); newton(0); newton(1)
+            if k == 0:
+                pick("s", T.Rw[:, R:2 * R], T.sndR[:, 1:2 * R:2], ["r2"], "sndR1")
+                small("R", "sndR", "Rw", 2 * R, 2 * H, ["sndR0", "sndR1"])
+                op("s", ["r2"], ["rq1"], lambda: S.activation(T.rq[:, R:2 * R], T.Rw[:, R:2 * R], Act.Square))
+                op("s", ["r2"], ["rr1"], lambda: S.activation(T.rr[:, R:2 * R], T.Rw[:, R:2 * R], Act.Identity, scale=2.0))
+            else:
+                dma("q", "st", 0, T.inv[:], T.r3[:], ["r3"], [])
+                stores[0] += 16
+        else:
+            low_init()
+            init_up(0); init_up(1)
+            G(1); G(0)
+            for v in range(2, 9):
+                G(v)
+            FL(0); FL(1); M(1); M(0); FL(2); M(2); F(3); M(3); F(4)
+            op("v", [dg, "P2"], ["Yl3"], lambda: V.tensor_tensor(T.Y[:, 3 * R:4 * R], T[dg][:, 0:R], T.P2[:, 2 * R:3 * R], Op.subtract))
+            init_up(2)
+            fin2(); fin01()
+            store(0, 4 * R, ["Yl0", "Yl2", "Yl3"])
+            M(4); F(5); M(5); fin(0); M(6); F(6); M(7); fin(1); M(8); F(7); F(8); fin(2)
+
+    stores = [0]
+    for k in range(3):
+        sweep(k)
+    for sem, n in count.items():
+        need("g", (sem, n))
+    need("g", ("sent", sent[0]))
+    need("g", ("st", stores[0]))

@@ -173,13 +173,13 @@ def rank_program(g, core, T, topo):
 
     op("v", [], ["colI"], lambda: V.memset(T.colI[:], 0))
     dma("q", "lship", 16, T.shipI[:], T.ship[:], [], ["shipI"])
-    dma("s", "lspot", 16, T.spotI[:], T.spot[:], [], ["spotI"])
     order("q", ["colI"], [])
     order("s", ["colI"], [])
     for k in range(8):
-        dma("qs"[k % 2], "lcol", 128, T.colI[16 * k:16 * k + 10, :], T.col[k, :], [], [])
+        dma("sq"[k % 2], "lcol", 128, T.colI[16 * k:16 * k + 10, :], T.col[k, :], [], [])
     wr["colI"] = ("lcol", 128)
     dma("q", "lup", 16, T.A[:, OWN:WIN], T.val[:, 4 * R:10 * R], [], ["Aup"])
+    dma("s", "lspot", 16, T.spotI[:], T.spot[:], [], ["spotI"])
     dma("s", "llow", 16, T.lowd[:], T.val[:, 0:4 * R], [], ["lowd"])
     op("g", [], ["ioJ"], lambda: g.iota(T.ioJ[:], [[-32, 4], [1000, 2], [-1, 16]], 0, 1, allow_small_or_imprecise_dtypes=True))
     op("g", [], ["ioK"], lambda: g.iota(T.ioK[:], [[-1, 128]], 0, 1, allow_small_or_imprecise_dtypes=True))
@@ -194,20 +194,14 @@ def rank_program(g, core, T, topo):
         op("v", ["W0"], ["W"], lambda: V.tensor_scalar(T.W[:, 512 * w:512 * w + 512], T.W0[:], float(LIFT + w + 1), None, Op.mult), True)
 
     weigh(0)
-    weigh(1)
 
     op("v", ["shipI"], ["shipU"], lambda: V.tensor_copy(T.shipU[:], T.shipI[:]))
     op("v", ["colI", "shipU"], ["sndC"], lambda: V.tensor_copy(T.sndC[:], T.colI[:, 0:R].indirect(T.shipU[:, 0:14])))
     small("C", "sndC", "colF", R, H, ["sndC"])
 
     op("v", ["colI"], ["colF"], lambda: V.tensor_copy(T.colF[:, 0:R], T.colI[:]))
-    op("v", ["spotI"], ["spotU"], lambda: V.tensor_copy(T.spotU[:], T.spotI[:]))
-    for v in range(3):
-        op("v", ["spotI"], ["spotF"], lambda: V.tensor_copy(T.spotF[:, 42 * v:42 * v + 42], T.spotI[:]), True)
+    weigh(1)
     op("v", ["colF"], ["colT"], lambda: V.transpose(T.colT[:], T.colF[:, 0:R]))
-    op("v", ["spotF"], ["lg"], lambda: V.tensor_scalar(T.lg[:], T.spotF[:], float(R), None, Op.is_ge))
-    for w in range(6):
-        op("s", ["colT"], ["rep"], lambda: S.activation(T.rep[:, :, :, w], T.colT[:, :, 0:10], Act.Copy), True)
 
     def pick(q, src, out, reads, res):
         src = src.indirect(T.shipU[:, 0:14])
@@ -224,17 +218,32 @@ def rank_program(g, core, T, topo):
     for c in range(3, 6):
         ship("s", "A", "sndA", c, ["Aup"])
     exchange(0, ["sndA%d" % c for c in range(6)])
+    for w in range(6):
+        op("s", ["colT"], ["rep"], lambda: S.activation(T.rep[:, :, :, w], T.colT[:, :, 0:10], Act.Copy), True)
+    op("v", ["spotI"], ["spotU"], lambda: V.tensor_copy(T.spotU[:], T.spotI[:]))
+    for v in range(3):
+        op("v", ["spotI"], ["spotF"], lambda: V.tensor_copy(T.spotF[:, 42 * v:42 * v + 42], T.spotI[:]), True)
+    weigh(2)
+    op("v", ["spotF"], ["lg"], lambda: V.tensor_scalar(T.lg[:], T.spotF[:], float(R), None, Op.is_ge))
+    weigh(3)
     own0, halo0 = OWN - R - LIFT * R, HALO - 1 - 6 * R - LIFT
     op("v", ["lg"], ["lm"], lambda: V.tensor_scalar(T.lm[:], T.lg[:], 5.0, 1.0, Op.mult, Op.add))
     op("v", ["lg"], ["strR"], lambda: V.tensor_scalar(T.strR[:], T.lg[:], float(1 - R), float(R), Op.mult, Op.add))
     op("v", ["lg"], ["lc"], lambda: V.tensor_scalar(T.lc[:], T.lg[:], float(halo0 - own0), float(own0), Op.mult, Op.add))
     op("v", ["lm", "spotF"], ["lm"], lambda: V.tensor_tensor(T.lm[:], T.lm[:], T.spotF[:], Op.mult))
-    weigh(2)
+    weigh(4)
     op("v", ["lm", "lc"], ["baseR"], lambda: V.tensor_tensor(T.baseR[:], T.lm[:], T.lc[:], Op.add))
-    for t, v0, v1, s0 in ((0, 0, 9, 1), (1, 0, 1, 0), (1, 1, 9, 2), (2, 0, 2, 0), (2, 2, 9, 3)):
-        op("s", ["rep"], ["rep3"], lambda: S.activation(T.rep3[:, 14 * t:14 * t + 14, v0:v1, :], T.rep[:, :, s0:s0 + v1 - v0, :], Act.Copy), True)
-    for w in range(3, 6):
-        weigh(w)
+    weigh(5)
+
+    def spread(q, t, v0, v1, s0):
+        out, src = T.rep3[:, 14 * t:14 * t + 14, v0:v1, :], T.rep[:, :, s0:s0 + v1 - v0, :]
+        if q == "v":
+            op("v", ["rep"], ["rep3v"], lambda: V.tensor_copy(out, src), True)
+        else:
+            op("s", ["rep"], ["rep3s"], lambda: S.activation(out, src, Act.Copy), True)
+
+    for job in (("s", 0, 0, 9, 1), ("s", 1, 0, 1, 0), ("s", 1, 1, 9, 2), ("v", 2, 0, 2, 0), ("v", 2, 2, 9, 3)):
+        spread(*job)
     op("v", ["ioK"], ["idB"], lambda: V.tensor_scalar(T.idB[:], T.ioK[:], 0.0, None, Op.is_equal))
     op("v", ["ioK"], ["idN"], lambda: V.tensor_scalar(T.idN[:], T.ioK[:], 0.0, -1.0, Op.is_equal, Op.mult))
     op("p", ["lowd", "idB"], ["X0"], lambda: P.matmul(T.X0[:, 0:2 * R], T.idB[:], T.lowd[:, 0:2 * R], True, True))
@@ -250,7 +259,7 @@ def rank_program(g, core, T, topo):
     pick("s", T.Rw[:, 0:R], T.sndR[:, 0:2 * R:2], ["r1"], "sndR0")
 
     def compare(v):
-        op("v", ["cut0", "cut1", "rep3"], ["eq%d" % v],
+        op("v", ["cut0", "cut1", "rep3s", "rep3v"], ["eq%d" % v],
            lambda: V.tensor_tensor(T.eq[:, 252 * v:252 * v + 252], T.cut[:, 0:42, 4:10], T.rep3[:, :, v, :], Op.is_equal))
 
     def fold(v0, bank):
@@ -278,11 +287,14 @@ def rank_program(g, core, T, topo):
     fold(3, "X1")
     compare(6)
     compare(7)
-    place(3, "X1", 0)
     compare(8)
-    place(3, "X1", 1)
     fold(6, "D")
+    place(3, "X1", 0)
+    compare(0)
+    place(3, "X1", 1)
+    place(6, "D", 0)
     place(3, "X1", 2)
+    place(6, "D", 1)
 
     def sweep(k):
         win = ("A", "U1", "U2")[k]
@@ -305,6 +317,8 @@ def rank_program(g, core, T, topo):
         def F(v):
             op("v", whole + [offs(v), x2n], ["P%d" % v], lambda: V.tensor_tensor(
                 T.P2[:, R * v:R * (v + 1)], T[win][:, 0:WIN].indirect(T.off[:, 42 * v + 28:42 * v + 42]), x2, Op.mult))
+            if v < 2:
+                sub(xn, v * R, T.P2[:, v * R:(v + 1) * R], "P%d" % v, False)
 
         def init(bank, src, n, res):
             op("p", [res, "idB"], [bank], lambda: P.matmul(T[bank][:, 0:n], T.idB[:], src, True, False))
@@ -333,8 +347,8 @@ def rank_program(g, core, T, topo):
                 sub(dg, 0, g_part(2, 0), res, False)
                 sub(dg, 0, g_part(2, 1), res, True)
 
-        def store(lo, hi, res):
-            dma("q", "st", 0, T.y[:, lo:hi], T.Y[:, lo:hi], res, [])
+        def store(q, lo, hi, res):
+            dma(q, "st", 0, T.y[:, lo:hi], T.Y[:, lo:hi], res, [])
             stores[0] += 16
 
         def init_up(i):
@@ -347,19 +361,17 @@ def rank_program(g, core, T, topo):
             op("v", ["B%d" % i, "P%d" % v, "P%d" % (v + 1)], [res],
                lambda: V.tensor_tensor(out, T["B%d" % i][:, 0:2 * R], T.P2[:, v * R:(v + 2) * R], Op.subtract))
             if not new:
-                store((4 + 2 * i) * R, (6 + 2 * i) * R, [res])
+                store("q", (4 + 2 * i) * R, (6 + 2 * i) * R, [res])
+
+        def fin_last(j):
+            op("v", ["B2", "P%d" % (7 + j)], ["Yz%d" % j], lambda: V.tensor_tensor(
+                T.Y[:, (8 + j) * R:(9 + j) * R], T.B2[:, j * R:(j + 1) * R], T.P2[:, (7 + j) * R:(8 + j) * R], Op.subtract))
+            store("qs"[j], (8 + j) * R, (9 + j) * R, ["Yz%d" % j])
 
         def low_init():
             init(xn, T.lowd[:, 0:2 * R], 2 * R, "lowd")
-            init("D", T.lowd[:, 2 * R:3 * R], R, "lowd")
             init(dg, diag, R, "lowd")
-
-        def FL(v):
-            F(v)
-            if v < 2:
-                sub(xn, v * R, T.P2[:, v * R:(v + 1) * R], "P%d" % v, False)
-            elif k < 2:
-                sub(dg, 0, T.P2[:, 2 * R:3 * R], "P2", False)
+            init("D", T.lowd[:, 2 * R:3 * R], R, "lowd")
 
         def fin2():
             out, res = (T.x2[:, k * R:(k + 1) * R], "x2%d" % k) if k < 2 else (T.Y[:, 2 * R:3 * R], "Yl2")
@@ -373,6 +385,10 @@ def rank_program(g, core, T, topo):
                 return
             out, res = (T[xn][:, 0:2 * R], xn) if k == 1 else (T.Y[:, 0:2 * R], "Yl0")
             op("v", [xn, "rg%d" % k], [res], lambda: V.tensor_tensor(out, T[xn][:, 0:2 * R], T.rg[:, rg:rg + 2 * R], Op.mult))
+
+        def fin3():
+            out, res = (T[dg][:, 0:R], dg) if k < 2 else (T.Y[:, 3 * R:4 * R], "Yl3")
+            op("v", [dg, "P2"], [res], lambda: V.tensor_tensor(out, T[dg][:, 0:R], T.P2[:, 2 * R:3 * R], Op.subtract))
 
         def newton(step):
             out, res = (T.Rw[:, R:2 * R], "r2") if k == 0 else (T.r3[:], "r3")
@@ -389,40 +405,33 @@ def rank_program(g, core, T, topo):
             for i in range(3):
                 init_up(i)
             G(3); G(4); G(5)
-            if k == 0:
-                place(6, "D", 0)
             F(3)
             if k == 0:
-                place(6, "D", 1)
-            F(4)
-            if k == 0:
                 place(6, "D", 2)
+            F(4)
             G(6); G(7); G(8)
-            M(3); M(4); F(5); M(5); fin(0); M(6); F(6); M(7)
+            M(3); M(4); F(5); M(5); M(6); fin(0); M(7); F(6); M(8)
             ship("s", new, snd, 0, [new + "u0"]); ship("s", new, snd, 1, [new + "u0"])
-            fin(1); M(8); F(7); F(8)
+            fin(1); F(7); F(8)
             ship("s", new, snd, 2, [new + "u1"]); ship("s", new, snd, 3, [new + "u1"])
-            if k == 1:
-                G(1)
             fin(2)
             ship("s", new, snd, 4, [new + "u2"]); ship("v", new, snd, 5, [new + "u2"])
             exchange(k + 1, [snd + str(c) for c in range(6)])
             if k == 0:
-                compare(0); compare(1); compare(2)
+                compare(1); compare(2)
                 fold(0, "X1")
                 op("v", ["lg"], ["lr0"], lambda: V.tensor_scalar(T.lr[:, 0:42], T.lg[:, 0:42], 1.0, None, Op.add))
-                place(0, "X1", 0)
                 op("v", ["lr0", "spotF"], ["lr0"], lambda: V.tensor_tensor(T.lr[:, 0:42], T.lr[:, 0:42], T.spotF[:, 0:42], Op.mult))
-                place(0, "X1", 1)
                 op("v", ["lr0", "strR"], ["lr1"], lambda: V.tensor_tensor(T.lr[:, 42:84], T.lr[:, 0:42], T.strR[:, 0:42], Op.add))
-                place(0, "X1", 2)
+                place(0, "X1", 0)
                 op("v", ["lr0", "lr1"], ["offR"], lambda: V.tensor_copy(T.offR[:], T.lr[:]))
-                G(1)
+                place(0, "X1", 1)
+                place(0, "X1", 2)
             low_init()
-            G(0); G(2)
+            G(2); G(1); G(0)
             if k == 1:
                 r_of_lower(0); r_of_lower(1)
-            FL(0); FL(1); M(1); M(0); FL(2); M(2); fin2(); fin01(); newton(0); newton(1)
+            F(0); F(1); M(2); F(2); M(1); fin3(); M(0); newton(0); fin2(); newton(1); fin01()
             if k == 0:
                 pick("s", T.Rw[:, R:2 * R], T.sndR[:, 1:2 * R:2], ["r2"], "sndR1")
                 small("R", "sndR", "Rw", 2 * R, 2 * H, ["sndR0", "sndR1"])
@@ -434,15 +443,14 @@ def rank_program(g, core, T, topo):
         else:
             low_init()
             init_up(0); init_up(1)
-            G(1); G(0)
-            for v in range(2, 9):
+            G(2); G(1); G(0)
+            for v in range(3, 9):
                 G(v)
-            FL(0); FL(1); M(1); M(0); FL(2); M(2); F(3); M(3); F(4)
-            op("v", [dg, "P2"], ["Yl3"], lambda: V.tensor_tensor(T.Y[:, 3 * R:4 * R], T[dg][:, 0:R], T.P2[:, 2 * R:3 * R], Op.subtract))
+            F(0); F(1); M(2); F(2); M(1); F(3); M(0); M(3); fin3()
             init_up(2)
-            fin2(); fin01()
-            store(0, 4 * R, ["Yl0", "Yl2", "Yl3"])
-            M(4); F(5); M(5); fin(0); M(6); F(6); M(7); fin(1); M(8); F(7); F(8); fin(2)
+            F(4); M(4); fin2(); F(5); M(5); fin01()
+            store("q", 0, 4 * R, ["Yl0", "Yl2", "Yl3"])
+            M(6); fin(0); M(7); F(6); M(8); fin(1); F(7); F(8); fin_last(0); fin_last(1)
 
     stores = [0]
     for k in range(3):

@@ -6,37 +6,55 @@ BLK = 6 * H
 HALO = 16
 OWN = HALO + NB * BLK
 WIN = OWN + 6 * R
-LIFT = 1400
-F32, BF, F16, I32, U16 = "float32", "bfloat16", "float16", "int32", "uint16"
+LIFT = 64
+F32, BF, I32, U16 = "float32", "bfloat16", "int32", "uint16"
 
 SCRATCH = {
-    "shipI": ("sbuf", [128, 14], I32), "shipU": ("sbuf", [128, 14], U16),
-    "spotI": ("sbuf", [128, 42], I32), "spotU": ("sbuf", [128, 42], U16), "spotF": ("sbuf", [128, 126], F32),
-    "lg": ("sbuf", [128, 126], F32), "lm": ("sbuf", [128, 126], F32), "lc": ("sbuf", [128, 126], F32),
-    "strR": ("sbuf", [128, 126], F32), "baseR": ("sbuf", [128, 126], F32), "jt": ("sbuf", [128, 378], F32),
-    "lr": ("sbuf", [128, 84], F32), "offR": ("sbuf", [128, 84], U16), "off": ("sbuf", [128, 378], U16),
+    "shipI": ("sbuf", [128, NB, 2], I32), "shipU": ("sbuf", [128, 14], U16), "shipW": ("sbuf", [128, NB, 6, 2], I32),
+    "ship2": ("sbuf", [128, 28], U16), "ship4": ("sbuf", [128, 56], U16), "ship6": ("sbuf", [128, 84], U16),
+    "spotI": ("sbuf", [128, 126], I32), "spotU": ("sbuf", [128, 42], U16), "spotF": ("sbuf", [128, 126], F32),
+    "hi": ("sbuf", [128, 126], I32), "lg": ("sbuf", [128, 126], F32), "stride": ("sbuf", [128, 126], F32),
+    "nbo": ("sbuf", [128, 126], F32), "d1": ("sbuf", [128, 126], F32), "d2": ("sbuf", [128, 126], F32),
+    "jt": ("sbuf", [128, 378], F32), "off": ("sbuf", [128, 378], U16),
     "colI": ("sbuf", [128, R], I32), "colF": ("sbuf", [128, 2 * R], F32), "sndC": ("sbuf", [128, R], F32),
-    "colT": ("sbuf", [128, 14, 16], F32), "rep": ("sbuf", [128, 14, 10, 6], F32), "rep3": ("sbuf", [128, 42, 9, 6], F32),
-    "cug": ("sbuf", [128, 3 * R], F32), "eq": ("sbuf", [128, 9 * 252], F16),
-    "ioJ": ("sbuf", [128, 128], F32), "ioK": ("sbuf", [128, 128], F32),
+    "colT": ("sbuf", [128, 14, 16], F32), "repU": ("sbuf", [128, 42, 7, 6], F32),
+    "rep0": ("sbuf", [128, 14, 3, 6], F32), "repL": ("sbuf", [128, 42, 2, 6], F32),
+    "cug": ("sbuf", [128, 3 * R], F32), "eq": ("sbuf", [128, 9 * 252], BF),
+    "ioJ": ("sbuf", [128, 128], BF), "ioK": ("sbuf", [128, 128], BF),
     "idB": ("sbuf", [128, 128], BF), "idN": ("sbuf", [128, 128], F32),
-    "W0": ("sbuf", [128, 512], F16), "W": ("sbuf", [128, 6 * 512], F16),
+    "W0": ("sbuf", [128, 512], BF), "W": ("sbuf", [128, 6 * 512], BF),
     "lowd": ("sbuf", [128, 4 * R], BF), "A": ("sbuf", [128, WIN], BF),
     "U1": ("sbuf", [128, WIN], F32), "U2": ("sbuf", [128, WIN], F32),
     "sndA": ("sbuf", [128, NB * BLK], BF), "snd1": ("sbuf", [128, NB * BLK], F32), "snd2": ("sbuf", [128, NB * BLK], F32),
     "relA": ("sbuf", [128, BLK], BF), "rel1": ("sbuf", [128, BLK], F32), "rel2": ("sbuf", [128, BLK], F32),
-    "Rw": ("sbuf", [128, 4 * R], F32), "sndR": ("sbuf", [128, 2 * R], F32),
-    "G": ("sbuf", [128, 9 * 2 * R], F32), "P2": ("sbuf", [128, 9 * R], F32),
-    "x2": ("sbuf", [128, 2 * R], F32), "rg": ("sbuf", [128, 6 * R], F32),
+    "relC": ("sbuf", [128, H], F32), "relD": ("sbuf", [128, H], BF), "relR": ("sbuf", [128, H], F32),
+    "Dw": ("sbuf", [128, 2 * R], BF), "sndD": ("sbuf", [128, R], BF),
+    "Rw": ("sbuf", [128, 2 * R], F32), "sndR": ("sbuf", [128, R], F32),
+    "G": ("sbuf", [128, 9, 3 * R], F32), "x2": ("sbuf", [128, 2 * R], F32), "rg": ("sbuf", [128, 6 * R], F32),
     "rq": ("sbuf", [128, 2 * R], F32), "rr": ("sbuf", [128, 2 * R], F32), "r3": ("sbuf", [128, R], F32),
     "Y": ("sbuf", [128, 10 * R], F32),
-    "cut": ("psum", [128, 64, 16], F32),
-    "X0": ("psum", [128, 512], F32), "X1": ("psum", [128, 512], F32), "D": ("psum", [128, 512], F32),
+    "XA": ("psum", [128, 64, 16], F32), "XB": ("psum", [128, 64, 16], F32), "J": ("psum", [128, 512], F32),
     "B0": ("psum", [128, 512], F32), "B1": ("psum", [128, 512], F32), "B2": ("psum", [128, 512], F32),
 }
-SEMAPHORES = ["cv", "cs", "cp", "cg", "lship", "lspot", "lcol", "lup", "llow", "st",
-              "arC", "arA", "ar1", "ar2", "arR", "hA", "h1", "h2", "sent"]
-ROUNDS = (("A", "sndA", "relA", "A"), ("1", "snd1", "rel1", "U1"), ("2", "snd2", "rel2", "U2"))
+CHUNKS = ((0, 2), (2, 4), (4, 6))
+SENDS = {"C": ("colF", R, H, 0, H), "A": ("A", HALO, BLK, 0, BLK), "D": ("Dw", R, H, 0, H)}
+for _k in (1, 2):
+    for _i, (_a, _b) in enumerate(CHUNKS):
+        SENDS["%d%d" % (_k, _i)] = ("U%d" % _k, HALO, BLK, H * _a, H * _b)
+    SENDS.setdefault("R", ("Rw", R, H, 0, H))
+DIRECT = "CDR"
+SHARE = ((0, 2), (2, 4), (0, 4))
+RELAYED = [n for n in SENDS if n not in DIRECT]
+SEMAPHORES = ["cv", "cs", "cp", "cg", "lship", "lspot", "lcol", "lup", "llow", "ldg", "st",
+              "arC", "arA", "ar1", "ar2", "arD", "arR", "sent"] + ["h" + n for n in RELAYED]
+
+ORDER = (
+    "e4 e3 e5 e2 l3 e6 l5 e7 a3 e8 b3 l7 G3 G4 e0 a5 F3 e1 b5 H5 iB1 l0 M3 a7 M4 b7 F4 G6 G7 a0 G8 N5 b0 f0 iB2 x0 M6 H1 "
+    "M7 F6 M8 f1 iL x1 F8 F7 N1 G2 f2 X2 M2 G0 iB1 F2 M0 d n0 c2 iB0 n1 F0 iB2 m rA r",
+    "G3 iL F5 G4 F3 M3 G5 F6 G6 M4 F4 M5 M6 f0 G7 F7 G8 M7 M8 x0 f1 F8 F2 G1 M1 iB0 x1 f2 G2 G0 X2 "
+    "rB M2 F1 M0 iB1 F0 d n0 m w c2 n1 iB2",
+    "G0 iL G1 G2 G3 F0 F1 H4 M0 F2 H5 M1 G6 F3 M2 M3 G8 w N4 d N5 F6 G7 M6 M8 y f0 M7 f1 F7 F8 z0 z1",
+)
 
 
 def bits(engines):
@@ -63,20 +81,25 @@ def routes(T, topo):
     return plan
 
 
-def landing(buf, lo, width, p, q):
-    b = p if p < q else p - 1
-    return buf[:, lo + b * width:lo + (b + 1) * width]
+def other(p, q):
+    return p if p < q else p - 1
+
+
+def landing(T, name, p, q):
+    win, lo, pitch, a, b = SENDS[name]
+    lo += other(p, q) * pitch
+    return T[win][:, lo + a:lo + b]
 
 
 def helper_program(g, core, T, topo, p, i, q):
     dst = T.cores[q]
     rid, pid = topo.addr(dst, core)
     n = len(topo.engines(core, dst))
-    got = n if i == 2 else n // 2
-    for name, _, rel, win in ROUNDS:
-        g.wait_ge(T.sem["h" + name], got)
-        g.remote_dma(landing(T[win], HALO, BLK, p, q), T[rel][:], T.sem["ar" + name], T.sem.sent, pid, rid, topo.mask(core, dst))
-    g.wait_ge(T.sem.sent, n * len(ROUNDS))
+    for name in RELAYED:
+        a, b = SENDS[name][3:]
+        g.wait_ge(T.sem["h" + name], (SHARE[i][1] - SHARE[i][0]) * n // 4)
+        g.remote_dma(landing(T, name, p, q), T["rel" + name[0]][:, a:b], T.sem["ar" + name[0]], T.sem.sent, pid, rid, topo.mask(core, dst))
+    g.wait_ge(T.sem.sent, n * len(RELAYED))
 
 
 def rank_program(g, core, T, topo):
@@ -102,14 +125,17 @@ def rank_program(g, core, T, topo):
             eng[q].wait_ge(T.sem[tok[0]], tok[1])
 
     def order(q, reads, writes, chain=False):
-        toks = {}
+        toks = []
         for r in reads:
-            if r in wr:
-                toks[wr[r][0]] = max(toks.get(wr[r][0], 0), wr[r][1])
+            toks += [wr[r]] if r in wr else []
+            toks += [t for t in rd.get(r, []) if r[0] == "#" and t[0] != "c" + q]
         for w in writes:
-            for t in rd.get(w, []) + ([wr[w]] if w in wr and not chain else []):
-                toks[t[0]] = max(toks.get(t[0], 0), t[1])
-        for t in toks.items():
+            toks += rd.get(w, [])
+            toks += [wr[w]] if w in wr and not (chain and wr[w][0] == "c" + q) else []
+        most = {}
+        for s, n in toks:
+            most[s] = max(most.get(s, 0), n)
+        for t in most.items():
             need(q, t)
 
     def mark(tok, reads, writes):
@@ -134,325 +160,298 @@ def rank_program(g, core, T, topo):
     off_chip = topo.engines(core, cores[direct[0]])
     on_chip = [e for e in topo.engines(core, relay[0][0]) if e not in off_chip]
     ne = len(off_chip)
-    sent = [0]
-
-    def piece(snd, width, q):
-        b = q if q < rank else q - 1
-        return T[snd][:, b * width:(b + 1) * width]
+    sent, stores, landed = [0], [0], {}
 
     def dst_id(c):
         rid, pid = topo.addr(c, core)
         return DstId(rid=rid, pnc=pid)
 
-    def exchange(k, reads):
-        name, snd, rel, win = ROUNDS[k]
+    def exchange(name, reads):
+        kind, (a, b) = name[0], SENDS[name][3:]
         order("g", reads, [])
-        d, h = ne // len(direct), len(on_chip) // 2
-        tr = [RemoteDMATransfer(dst_ids=[dst_id(cores[q])], dma_engine_mask=bits(off_chip[i * d:(i + 1) * d]),
-                                remote_sem=T.sem["ar" + name], src=piece(snd, BLK, q), dst=landing(T[win], HALO, BLK, rank, q))
-              for i, q in enumerate(direct)]
-        tr += [RemoteDMATransfer(dst_ids=[dst_id(c)], dma_engine_mask=bits(on_chip[i * h:(i + 1) * h]),
-                                 remote_sem=T.sem["h" + name], src=piece(snd, BLK, q), dst=T[rel][:])
-               for i, (c, q) in enumerate(relay[:2])]
-        g.remote_dma_fused(tr, local_sem=T.sem.sent)
-        c, q = relay[2]
-        rid, pid = topo.addr(c, core)
-        g.remote_dma(T[rel][:], piece(snd, BLK, q), T.sem["h" + name], T.sem.sent, pid, rid, bits(on_chip))
-        sent[0] += ne + 2 * len(on_chip)
-        wr["halo" + name] = ("ar" + name, ne + ne * len(relay))
 
-    def small(name, snd, buf, lo, width, reads):
-        order("g", reads, [])
-        to = direct + [q for _, q in relay]
-        g.remote_dma_fused([RemoteDMATransfer(dst_ids=[dst_id(cores[q])], dma_engine_mask=bits(off_chip[i:i + 1]),
-                                              remote_sem=T.sem["ar" + name], src=piece(snd, width, q),
-                                              dst=landing(T[buf], lo, width, rank, q)) for i, q in enumerate(to)],
-                           local_sem=T.sem.sent)
-        sent[0] += len(to)
-        wr["halo" + name] = ("ar" + name, len(to))
+        def piece(q):
+            lo = NB * a + other(q, rank) * (b - a)
+            return T["snd" + kind][:, lo:lo + b - a]
+
+        to = direct + [q for _, q in relay] * (name in DIRECT)
+        d, h = ne // len(to), len(on_chip) // 4
+        jobs = [(off_chip[i * d:(i + 1) * d], cores[q], "ar" + kind, piece(q), landing(T, name, rank, q)) for i, q in enumerate(to)]
+        got = d * len(to)
+        if name not in DIRECT:
+            jobs += [(on_chip[lo * h:hi * h], c, "h" + name, piece(q), T["rel" + kind][:, a:b]) for (lo, hi), (c, q) in zip(SHARE, relay)]
+            got += ne * len(relay)
+        while jobs:
+            call, busy = [], []
+            while jobs and not set(jobs[0][0]) & set(busy):
+                es, c, sem, src, dst = jobs.pop(0)
+                busy += es
+                call.append(RemoteDMATransfer(dst_ids=[dst_id(c)], dma_engine_mask=bits(es), remote_sem=T.sem[sem], src=src, dst=dst))
+            g.remote_dma_fused(call, local_sem=T.sem.sent)
+            sent[0] += len(busy)
+        landed[kind] = landed.get(kind, 0) + got
+        wr["halo" + kind] = ("ar" + kind, landed[kind])
+
+    def scaled(out, src, mul, add):
+        op("v", [src], [out], lambda: V.tensor_scalar(T[out][:], T[src][:], float(mul), float(add), Op.mult, Op.add))
+
+    def copy(q, out, src, reads, writes, chain=False):
+        op(q, reads, writes, (lambda: V.tensor_copy(out, src)) if q == "v" else (lambda: S.activation(out, src, Act.Copy)), chain)
+
+    def pick(q, src, out, reads, res):
+        copy(q, out, src.indirect(T.shipU[:, 0:14]), reads + ["shipU"], [res])
+
+    def ship(qs, win, snd, a, b, reads):
+        n, lst = b - a, "ship%d" % (b - a)
+        for i, q in enumerate(qs):
+            lo, hi = 14 * n * i // len(qs) // 2 * 2, 14 * n * (i + 1) // len(qs) // 2 * 2
+            copy(q, T[snd][:, a * R + 16 * lo:a * R + 16 * hi], T[win][:, OWN + a * R:OWN + b * R].indirect(T[lst][:, lo:hi]),
+                 reads + [lst], ["%s%d%s" % (snd, a, q)])
+        return ["%s%d%s" % (snd, a, q) for q in qs]
 
     op("v", [], ["colI"], lambda: V.memset(T.colI[:], 0))
     dma("q", "lship", 16, T.shipI[:], T.ship[:], [], ["shipI"])
+    dma("s", "lspot", 48, T.spotI[:, 0:42], T.spot[:], [], [])
     order("q", ["colI"], [])
     order("s", ["colI"], [])
     for k in range(8):
         dma("sq"[k % 2], "lcol", 128, T.colI[16 * k:16 * k + 10, :], T.col[k, :], [], [])
     wr["colI"] = ("lcol", 128)
-    dma("q", "lup", 16, T.A[:, OWN:WIN], T.val[:, 4 * R:10 * R], [], ["Aup"])
-    dma("s", "lspot", 16, T.spotI[:], T.spot[:], [], ["spotI"])
-    dma("s", "llow", 16, T.lowd[:], T.val[:, 0:4 * R], [], ["lowd"])
-    op("g", [], ["ioJ"], lambda: g.iota(T.ioJ[:], [[-32, 4], [1000, 2], [-1, 16]], 0, 1, allow_small_or_imprecise_dtypes=True))
+    dma("s", "lup", 16, T.A[:, OWN:WIN], T.val[:, 4 * R:10 * R], [], ["Aup"])
+    for v in (1, 2):
+        dma("q", "lspot", 48, T.spotI[:, 42 * v:42 * v + 42], T.spot[:], [], ["spotI"] if v == 2 else [])
+    dma("q", "ldg", 16, T.Dw[:, 0:R], T.val[:, 3 * R:4 * R], [], ["Dw"])
+    dma("q", "llow", 16, T.lowd[:], T.val[:, 0:4 * R], [], ["lowd"])
+    op("g", [], ["ioJ"], lambda: g.iota(T.ioJ[:], [[-32, 4], [128, 2], [-1, 16]], 0, 1, allow_small_or_imprecise_dtypes=True))
     op("g", [], ["ioK"], lambda: g.iota(T.ioK[:], [[-1, 128]], 0, 1, allow_small_or_imprecise_dtypes=True))
     for win in ("A", "U1", "U2"):
         op("v", [], [win + "z"], lambda: V.memset(T[win][:, 0:HALO], 0.0))
     for h in range(2):
         for e in range(2):
             lo = (2 * h + e) * 128
-            op("v", ["ioJ"], ["W0"], lambda: V.tensor_scalar(T.W0[:, lo:lo + 128], T.ioJ[:], float(16 * h + 1000 * e), None, Op.is_equal), True)
-
-    def weigh(w):
-        op("v", ["W0"], ["W"], lambda: V.tensor_scalar(T.W[:, 512 * w:512 * w + 512], T.W0[:], float(LIFT + w + 1), None, Op.mult), True)
-
-    weigh(0)
-
-    op("v", ["shipI"], ["shipU"], lambda: V.tensor_copy(T.shipU[:], T.shipI[:]))
-    op("v", ["colI", "shipU"], ["sndC"], lambda: V.tensor_copy(T.sndC[:], T.colI[:, 0:R].indirect(T.shipU[:, 0:14])))
-    small("C", "sndC", "colF", R, H, ["sndC"])
-
-    op("v", ["colI"], ["colF"], lambda: V.tensor_copy(T.colF[:, 0:R], T.colI[:]))
-    weigh(1)
-    op("v", ["colF"], ["colT"], lambda: V.transpose(T.colT[:], T.colF[:, 0:R]))
-
-    def pick(q, src, out, reads, res):
-        src = src.indirect(T.shipU[:, 0:14])
-        if q == "v":
-            op("v", reads + ["shipU"], [res], lambda: V.tensor_copy(out, src))
-        else:
-            op("s", reads + ["shipU"], [res], lambda: S.activation(out, src, Act.Copy))
-
-    def ship(q, win, snd, c, reads):
-        pick(q, T[win][:, OWN + c * R:OWN + (c + 1) * R], T[snd][:, c:NB * BLK:6], reads, snd + str(c))
-
-    for c in range(3):
-        ship("v", "A", "sndA", c, ["Aup"])
-    for c in range(3, 6):
-        ship("s", "A", "sndA", c, ["Aup"])
-    exchange(0, ["sndA%d" % c for c in range(6)])
-    for w in range(6):
-        op("s", ["colT"], ["rep"], lambda: S.activation(T.rep[:, :, :, w], T.colT[:, :, 0:10], Act.Copy), True)
-    op("v", ["spotI"], ["spotU"], lambda: V.tensor_copy(T.spotU[:], T.spotI[:]))
-    for v in range(3):
-        op("v", ["spotI"], ["spotF"], lambda: V.tensor_copy(T.spotF[:, 42 * v:42 * v + 42], T.spotI[:]), True)
-    weigh(2)
-    op("v", ["spotF"], ["lg"], lambda: V.tensor_scalar(T.lg[:], T.spotF[:], float(R), None, Op.is_ge))
-    weigh(3)
-    own0, halo0 = OWN - R - LIFT * R, HALO - 1 - 6 * R - LIFT
-    op("v", ["lg"], ["lm"], lambda: V.tensor_scalar(T.lm[:], T.lg[:], 5.0, 1.0, Op.mult, Op.add))
-    op("v", ["lg"], ["strR"], lambda: V.tensor_scalar(T.strR[:], T.lg[:], float(1 - R), float(R), Op.mult, Op.add))
-    op("v", ["lg"], ["lc"], lambda: V.tensor_scalar(T.lc[:], T.lg[:], float(halo0 - own0), float(own0), Op.mult, Op.add))
-    op("v", ["lm", "spotF"], ["lm"], lambda: V.tensor_tensor(T.lm[:], T.lm[:], T.spotF[:], Op.mult))
-    weigh(4)
-    op("v", ["lm", "lc"], ["baseR"], lambda: V.tensor_tensor(T.baseR[:], T.lm[:], T.lc[:], Op.add))
-    weigh(5)
-
-    def spread(q, t, v0, v1, s0):
-        out, src = T.rep3[:, 14 * t:14 * t + 14, v0:v1, :], T.rep[:, :, s0:s0 + v1 - v0, :]
-        if q == "v":
-            op("v", ["rep"], ["rep3v"], lambda: V.tensor_copy(out, src), True)
-        else:
-            op("s", ["rep"], ["rep3s"], lambda: S.activation(out, src, Act.Copy), True)
-
-    for job in (("s", 0, 0, 9, 1), ("s", 1, 0, 1, 0), ("s", 1, 1, 9, 2), ("v", 2, 0, 2, 0), ("v", 2, 2, 9, 3)):
-        spread(*job)
+            op("v", ["ioJ"], ["W0"], lambda: V.tensor_scalar(T.W0[:, lo:lo + 128], T.ioJ[:], float(16 * h + 128 * e), None, Op.is_equal), True)
     op("v", ["ioK"], ["idB"], lambda: V.tensor_scalar(T.idB[:], T.ioK[:], 0.0, None, Op.is_equal))
     op("v", ["ioK"], ["idN"], lambda: V.tensor_scalar(T.idN[:], T.ioK[:], 0.0, -1.0, Op.is_equal, Op.mult))
-    op("p", ["lowd", "idB"], ["X0"], lambda: P.matmul(T.X0[:, 0:2 * R], T.idB[:], T.lowd[:, 0:2 * R], True, True))
+    for w, q in enumerate("vvsvss"):
+        out = T.W[:, 512 * w:512 * w + 512]
+        if q == "s":
+            op("s", ["W0"], ["W%d" % w], lambda: S.activation(out, T.W0[:], Act.Identity, scale=float(LIFT + w)))
+        else:
+            op("v", ["W0"], ["W%d" % w], lambda: V.tensor_scalar(out, T.W0[:], float(LIFT + w), None, Op.mult))
 
-    op("s", ["colF", "haloC", "spotU"], ["cug1"], lambda: S.activation(T.cug[:, R:3 * R], T.colF[:, 0:2 * R].indirect(T.spotU[:, 14:42]), Act.Copy))
-    op("v", ["colF", "haloC", "spotU"], ["cug0"], lambda: V.tensor_copy(T.cug[:, 0:R], T.colF[:, 0:2 * R].indirect(T.spotU[:, 0:14])))
-    op("v", ["cug0"], ["cut0"], lambda: V.transpose(T.cut[:, 0:14, :], T.cug[:, 0:R]))
-    op("v", ["cug1"], ["cut1"], lambda: V.transpose(T.cut[:, 14:42, :], T.cug[:, R:3 * R]))
+    copy("v", T.shipU[:], T.shipI[:], ["shipI"], ["shipU"])
+    for w in range(3):
+        op("v", ["shipI"], ["shipW"], lambda: V.tensor_scalar(T.shipW[:, :, w, :], T.shipI[:], float(w * R), None, Op.add), True)
+    pick("v", T.colI[:, 0:R], T.sndC[:], ["colI"], "sndC")
+    exchange("C", ["sndC"])
+    op("v", ["shipW"], ["shipX"], lambda: V.tensor_scalar(T.shipW[:, :, 3:6, :], T.shipW[:, :, 0:3, :], float(3 * R), None, Op.add))
+    copy("v", T.colF[:, 0:R], T.colI[:], ["colI"], ["colF"])
+    copy("v", T.ship6[:], T.shipW[:], ["shipW", "shipX"], ["ship6"])
+    op("v", ["colF"], ["colT"], lambda: V.transpose(T.colT[:], T.colF[:, 0:R]))
+    exchange("A", ship("vs", "A", "sndA", 0, 6, ["Aup"]))
+    for n in sorted(set(b - a for a, b in CHUNKS) - {6}):
+        copy("v", T["ship%d" % n][:], T.shipW[:, :, 0:n, :], ["shipW", "shipX"], ["ship%d" % n])
+
+    copy("v", T.spotU[:], T.spotI[:, 0:42], ["spotI"], ["spotU"])
+    copy("v", T.spotF[:], T.spotI[:], ["spotI"], ["spotF"])
+    op("v", ["spotI"], ["hi"], lambda: V.tensor_scalar(T.hi[:], T.spotI[:], 512 - H, None, Op.bitwise_and))
+    op("v", ["spotF"], ["lg"], lambda: V.tensor_scalar(T.lg[:], T.spotF[:], float(R), None, Op.is_ge))
+    scaled("d2", "spotF", 1.0 / R - 1.0 / H, 0.0)
+    scaled("d1", "hi", -5.0 / H, (6 * R - HALO - 0.25) / H + (OWN + 0.25) / R)
+    scaled("nbo", "spotF", -1.0 / R, LIFT - (OWN + 0.25) / R)
+    op("v", ["d1", "d2"], ["d1"], lambda: V.tensor_tensor(T.d1[:], T.d1[:], T.d2[:], Op.add))
+    scaled("stride", "lg", H - R, R)
+    op("v", ["d1", "lg"], ["d1"], lambda: V.tensor_tensor(T.d1[:], T.d1[:], T.lg[:], Op.mult))
+    for w in range(6):
+        copy("s", T.repU[:, 0:14, :, w], T.colT[:, :, 3:10], ["colT"], ["repU0"], True)
+    copy("s", T.repU[:, 14:28, :, :], T.repU[:, 0:14, :, :], ["repU0"], ["repU1"])
+    copy("v", T.repU[:, 28:42, :, :], T.repU[:, 0:14, :, :], ["repU0"], ["repU2"])
+    pick("s", T.Dw[:, 0:R], T.sndD[:], ["Dw"], "sndD")
+    exchange("D", ["sndD"])
+
+    def init(bank, out, src, res):
+        op("p", [res, "idB"], [bank], lambda: P.matmul(out, T.idB[:], src, True, False))
+
+    def init_up(i):
+        init("#B%d" % i, T["B%d" % i][:, 0:2 * R], T.A[:, OWN + 2 * i * R:OWN + (2 * i + 2) * R], "Aup")
+
+    def start(bank, n):
+        op("p", ["nbo", "idN"], ["#" + bank], lambda: P.matmul(T[bank][:, 0:42 * n], T.idN[:], T.nbo[:, 0:42 * n], True, False))
+        op("p", ["d1"], ["#" + bank], lambda: P.matmul(T[bank][:, 0:42 * n], T.idN[:], T.d1[:, 0:42 * n], False, False), True)
+
+    op("p", ["lowd", "idB"], ["#XA0"], lambda: P.matmul(T.XA[:, 4:32, :], T.idB[:], T.lowd[:, 0:2 * R], True, True))
+    op("p", ["lowd", "idB"], ["#XA1"], lambda: P.matmul(T.XA[:, 32:46, :], T.idB[:], T.lowd[:, 2 * R:3 * R], True, True))
+    init_up(0)
+    for bank in ("J", "B1", "B2"):
+        start(bank, 2)
+
+    for t, q in enumerate("vss"):
+        copy(q, T.cug[:, t * R:(t + 1) * R], T.colF[:, 0:2 * R].indirect(T.spotU[:, 14 * t:14 * t + 14]),
+             ["colF", "haloC", "spotU"], ["cug%d" % t])
+    for t in range(3):
+        op("v", ["cug%d" % t], ["#XB0", "#XB1"], lambda: V.transpose(T.XB[:, 14 * t:14 * t + 14, :], T.cug[:, t * R:(t + 1) * R]), True)
     diag = T.lowd[:, 3 * R:4 * R]
-    op("s", ["lowd"], ["r1"], lambda: S.activation(T.Rw[:, 0:R], diag, Act.Identity, bias=2.0, scale=-1.0))
     op("s", ["lowd"], ["rq0"], lambda: S.activation(T.rq[:, 0:R], diag, Act.Square, bias=2.0, scale=-1.0))
     op("s", ["lowd"], ["rr0"], lambda: S.activation(T.rr[:, 0:R], diag, Act.Identity, bias=4.0, scale=-2.0))
-    pick("s", T.Rw[:, 0:R], T.sndR[:, 0:2 * R:2], ["r1"], "sndR0")
+    for w in range(6):
+        copy("s", T.rep0[:, :, :, w], T.colT[:, :, 0:3], ["colT"], ["rep0"], True)
+    for t, s in enumerate((slice(1, 3), slice(0, 3, 2), slice(0, 2))):
+        copy("s", T.repL[:, 14 * t:14 * t + 14, :, :], T.rep0[:, :, s, :], ["rep0"], ["repL"], True)
 
     def compare(v):
-        op("v", ["cut0", "cut1", "rep3s", "rep3v"], ["eq%d" % v],
-           lambda: V.tensor_tensor(T.eq[:, 252 * v:252 * v + 252], T.cut[:, 0:42, 4:10], T.rep3[:, :, v, :], Op.is_equal))
+        rep, res = (T.repL[:, :, v, :], ["repL"]) if v < 2 else (T.repU[:, :, v - 2, :], ["repU0", "repU1", "repU2"])
+        op("v", ["#XB0", "#XB1"] + res, ["eq%d" % v],
+           lambda: V.tensor_tensor(T.eq[:, 252 * v:252 * v + 252], T.XB[:, 0:42, 4:10], rep, Op.is_equal))
 
-    def fold(v0, bank):
-        first = True
+    def fold(v0, n, bank):
         for h in range(2):
             for i in range(12):
                 w, e = i // 2, i % 2
                 lo = 512 * w + (2 * h + e) * 128
-                op("p", ["eq%d" % v for v in range(v0, v0 + 3)] + ["W"], [bank],
-                   lambda: P.matmul(T[bank][:, h:126:2], T.W[:, lo:lo + 128],
-                                    T.eq[:, 252 * v0 + 6 * e + w:252 * v0 + 756:12], i == 0, i == 11), not first)
-                first = False
+                op("p", ["eq%d" % v for v in range(v0, v0 + n)] + ["W%d" % w], ["#" + bank],
+                   lambda: P.matmul(T[bank][:, h:42 * n:2], T.W[:, lo:lo + 128],
+                                    T.eq[:, 252 * v0 + 6 * e + w:252 * (v0 + n):12], False, h == 1 and i == 11), True)
 
-    def place(v0, bank, step):
-        a = 42 * v0
+    def place(v0, n, bank, step):
+        a, b = 42 * v0, 42 * (v0 + n)
         if step == 0:
-            op("v", [bank, "strR"], [bank], lambda: V.tensor_tensor(T[bank][:, 0:126], T[bank][:, 0:126], T.strR[:], Op.mult))
-        elif step == 1:
-            op("v", [bank, "baseR"], ["jt%d" % v0], lambda: V.tensor_tensor(T.jt[:, a:a + 126], T[bank][:, 0:126], T.baseR[:], Op.add))
+            op("v", ["#" + bank, "stride"], ["jt%d" % v0], lambda: V.tensor_tensor(T.jt[:, a:b], T[bank][:, 0:b - a], T.stride[:, 0:b - a], Op.mult))
         else:
-            op("v", ["jt%d" % v0], ["off%d" % v0], lambda: V.tensor_copy(T.off[:, a:a + 126], T.jt[:, a:a + 126]))
+            copy("v", T.off[:, a:b], T.jt[:, a:b], ["jt%d" % v0], ["off%d" % v for v in range(v0, v0 + n)])
 
-    for v in (3, 4, 5):
-        compare(v)
-    fold(3, "X1")
-    compare(6)
-    compare(7)
-    compare(8)
-    fold(6, "D")
-    place(3, "X1", 0)
-    compare(0)
-    place(3, "X1", 1)
-    place(6, "D", 0)
-    place(3, "X1", 2)
-    place(6, "D", 1)
+    groups = {3: (3, 2, "J"), 5: (5, 2, "B1"), 7: (7, 2, "B2"), 0: (0, 3, "J")}
 
     def sweep(k):
-        win = ("A", "U1", "U2")[k]
-        new = ("U1", "U2", None)[k]
-        snd = ("snd1", "snd2", None)[k]
+        win, new, snd = ("A", "U1", "U2")[k], ("U1", "U2", None)[k], ("snd1", "snd2", None)[k]
         whole = [win + "z", "halo" + "A12"[k]] + (["Aup"] if k == 0 else [win + "u%d" % i for i in range(3)])
-        xo, xn = ("X0", "X1", "X0")[k], ("X1", "X0", "X1")[k]
-        dg = "B2" if k == 2 else "B0"
-        x2 = T.lowd[:, 2 * R:3 * R] if k == 0 else T.x2[:, (k - 1) * R:k * R]
-        x2n = "lowd" if k == 0 else "x2%d" % (k - 1)
-        rg = (k - 1) * 3 * R
+        xo, xn = ("XA", "XB", "XA")[k], ("XB", "XA", "XB")[k]
+        x2, x2n = (T.lowd[:, 2 * R:3 * R], "lowd") if k == 0 else (T.x2[:, (k - 1) * R:k * R], "x2%d" % (k - 1))
+        dg, merged = T.J[:, 0:R], "m" in ORDER[k]
 
-        def offs(v):
-            return "off%d" % (v // 3 * 3)
+        def gather(v, n):
+            op("s", whole + ["off%d" % v], ["G%d" % v] + ["P%d" % v] * (n - 2), lambda: S.activation(
+                T.G[:, v, 0:n * R], T[win][:, 0:WIN].indirect(T.off[:, 42 * v:42 * v + 14 * n]), Act.Copy))
 
-        def G(v):
-            op("s", whole + [offs(v)], ["G%d" % v], lambda: S.activation(
-                T.G[:, 2 * R * v:2 * R * (v + 1)], T[win][:, 0:WIN].indirect(T.off[:, 42 * v:42 * v + 28]), Act.Copy))
-
-        def F(v):
-            op("v", whole + [offs(v), x2n], ["P%d" % v], lambda: V.tensor_tensor(
-                T.P2[:, R * v:R * (v + 1)], T[win][:, 0:WIN].indirect(T.off[:, 42 * v + 28:42 * v + 42]), x2, Op.mult))
-            if v < 2:
-                sub(xn, v * R, T.P2[:, v * R:(v + 1) * R], "P%d" % v, False)
-
-        def init(bank, src, n, res):
-            op("p", [res, "idB"], [bank], lambda: P.matmul(T[bank][:, 0:n], T.idB[:], src, True, False))
-
-        def sub(bank, lo, src, res, stop):
-            op("p", [res, "idN"], [bank], lambda: P.matmul(T[bank][:, lo:lo + R], T.idN[:], src, False, stop), True)
-
-        def g_part(v, t):
-            return T.G[:, (2 * v + t) * R:(2 * v + t + 1) * R]
-
-        def M(v):
-            gv = T.G[:, 2 * R * v:2 * R * (v + 1)]
-            res = "G%d" % v
-            op("v", [res, xo], [res], lambda: V.tensor_tensor(gv, gv, T[xo][:, 0:2 * R], Op.mult))
+        def target(v, t):
             if v >= 3:
                 i, j = (v - 3) // 2, (v - 3) % 2
-                sub("B%d" % i, j * R, g_part(v, 0), res, False)
-                sub("B%d" % i, j * R, g_part(v, 1), res, j == 1)
-            elif v == 0:
-                sub(xn, R, g_part(0, 0), res, False)
-                sub(xn, 0, g_part(0, 1), res, True)
-            elif v == 1:
-                sub("D", 0, g_part(1, 0), res, False)
-                sub("D", 0, g_part(1, 1), res, True)
-            else:
-                sub(dg, 0, g_part(2, 0), res, False)
-                sub(dg, 0, g_part(2, 1), res, True)
+                return "#B%d" % i, T["B%d" % i][:, j * R:(j + 1) * R]
+            if v == 2:
+                return "#J", dg
+            s = [s for s in range(3) if s != t][v]
+            return "#%s%d" % (xn, s // 2), T[xn][:, 4 + 14 * s:18 + 14 * s, :]
 
-        def store(q, lo, hi, res):
-            dma(q, "st", 0, T.y[:, lo:hi], T.Y[:, lo:hi], res, [])
+        def sub(v, t, res):
+            bank, out = target(v, t)
+            left[bank] -= 1
+            op("p", [res, "idN"], [bank], lambda: P.matmul(out, T.idN[:], T.G[:, v, t * R:(t + 1) * R], False, left[bank] == 0), True)
+
+        def fused(v):
+            op("v", whole + ["off%d" % v, x2n], ["P%d" % v], lambda: V.tensor_tensor(
+                T.G[:, v, 2 * R:3 * R], T[win][:, 0:WIN].indirect(T.off[:, 42 * v + 28:42 * v + 42]), x2, Op.mult))
+            if v < 2 and not merged:
+                sub(v, 2, "P%d" % v)
+
+        def times(v, n):
+            gv, res = T.G[:, v, 0:n * R], ["G%d" % v] + ["P%d" % v] * (n - 2)
+            op("v", res + ["#%s%d" % (xo, j) for j in range(n - 1)], res,
+               lambda: V.tensor_tensor(gv, gv, T[xo][:, 4:4 + 14 * n, :], Op.mult))
+            for t in range(n if v < 2 and not merged else 2):
+                sub(v, t, res[0])
+
+        def store(q, out, src, res):
+            dma(q, "st", 0, out, src, res, [])
             stores[0] += 16
 
-        def init_up(i):
-            init("B%d" % i, T.A[:, OWN + 2 * i * R:OWN + (2 * i + 2) * R], 2 * R, "Aup")
-
-        def fin(i):
-            v = 3 + 2 * i
-            out = T[new][:, OWN + 2 * i * R:OWN + (2 * i + 2) * R] if new else T.Y[:, (4 + 2 * i) * R:(6 + 2 * i) * R]
-            res = (new or "Y") + "u%d" % i
-            op("v", ["B%d" % i, "P%d" % v, "P%d" % (v + 1)], [res],
-               lambda: V.tensor_tensor(out, T["B%d" % i][:, 0:2 * R], T.P2[:, v * R:(v + 2) * R], Op.subtract))
+        def fin(i, j0, j1, q):
+            lo, hi = (2 * i + j0) * R, (2 * i + j1) * R
+            out = T[new][:, OWN + lo:OWN + hi] if new else T.Y[:, 4 * R + lo:4 * R + hi]
+            res = (new + "u%d" % i) if new else "Y%d" % lo
+            op("v", ["#B%d" % i] + ["P%d" % (3 + 2 * i + j) for j in range(j0, j1)], [res], lambda: V.tensor_tensor(
+                out, T["B%d" % i][:, j0 * R:j1 * R], T.G[:, 3 + 2 * i + j0:3 + 2 * i + j1, 2 * R:3 * R], Op.subtract))
             if not new:
-                store("q", (4 + 2 * i) * R, (6 + 2 * i) * R, [res])
+                store(q, T.y[:, 4 * R + lo:4 * R + hi], out, [res])
 
-        def fin_last(j):
-            op("v", ["B2", "P%d" % (7 + j)], ["Yz%d" % j], lambda: V.tensor_tensor(
-                T.Y[:, (8 + j) * R:(9 + j) * R], T.B2[:, j * R:(j + 1) * R], T.P2[:, (7 + j) * R:(8 + j) * R], Op.subtract))
-            store("qs"[j], (8 + j) * R, (9 + j) * R, ["Yz%d" % j])
+        def init_low():
+            init("#%s0" % xn, T[xn][:, 4:32, :], T.lowd[:, 0:2 * R], "lowd")
+            init("#%s1" % xn, T[xn][:, 32:46, :], T.lowd[:, 2 * R:3 * R], "lowd")
+            init("#J", dg, diag, "lowd")
 
-        def low_init():
-            init(xn, T.lowd[:, 0:2 * R], 2 * R, "lowd")
-            init(dg, diag, R, "lowd")
-            init("D", T.lowd[:, 2 * R:3 * R], R, "lowd")
-
-        def fin2():
-            out, res = (T.x2[:, k * R:(k + 1) * R], "x2%d" % k) if k < 2 else (T.Y[:, 2 * R:3 * R], "Yl2")
-            if k == 0:
-                op("v", ["D"], [res], lambda: V.tensor_copy(out, T.D[:, 0:R]))
-            else:
-                op("v", ["D", "rg%d" % k], [res], lambda: V.tensor_tensor(out, T.D[:, 0:R], T.rg[:, rg + 2 * R:rg + 3 * R], Op.mult))
-
-        def fin01():
-            if k == 0:
-                return
-            out, res = (T[xn][:, 0:2 * R], xn) if k == 1 else (T.Y[:, 0:2 * R], "Yl0")
-            op("v", [xn, "rg%d" % k], [res], lambda: V.tensor_tensor(out, T[xn][:, 0:2 * R], T.rg[:, rg:rg + 2 * R], Op.mult))
-
-        def fin3():
-            out, res = (T[dg][:, 0:R], dg) if k < 2 else (T.Y[:, 3 * R:4 * R], "Yl3")
-            op("v", [dg, "P2"], [res], lambda: V.tensor_tensor(out, T[dg][:, 0:R], T.P2[:, 2 * R:3 * R], Op.subtract))
+        def diagonal():
+            out, res = (dg, "#J") if k < 2 else (T.Y[:, 3 * R:4 * R], "Yd")
+            op("v", ["#J", "P2"], [res], lambda: V.tensor_tensor(out, dg, T.G[:, 2, 2 * R:3 * R], Op.subtract))
 
         def newton(step):
-            out, res = (T.Rw[:, R:2 * R], "r2") if k == 0 else (T.r3[:], "r3")
             if step == 0:
-                op("v", [dg, "rq%d" % k], [dg], lambda: V.tensor_tensor(T[dg][:, 0:R], T[dg][:, 0:R], T.rq[:, k * R:(k + 1) * R], Op.mult))
-            else:
-                op("v", [dg, "rr%d" % k], [res], lambda: V.tensor_tensor(out, T.rr[:, k * R:(k + 1) * R], T[dg][:, 0:R], Op.subtract))
-
-        def r_of_lower(j):
-            op("s", ["r1", "r2", "haloR", "offR"], ["rg%d" % (j + 1)], lambda: S.activation(
-                T.rg[:, 3 * R * j:3 * R * (j + 1)], T.Rw[:, 0:4 * R].indirect(T.offR[:, 42 * j:42 * j + 42]), Act.Copy))
-
-        if k < 2:
-            for i in range(3):
-                init_up(i)
-            G(3); G(4); G(5)
-            F(3)
-            if k == 0:
-                place(6, "D", 2)
-            F(4)
-            G(6); G(7); G(8)
-            M(3); M(4); F(5); M(5); M(6); fin(0); M(7); F(6); M(8)
-            ship("s", new, snd, 0, [new + "u0"]); ship("s", new, snd, 1, [new + "u0"])
-            fin(1); F(7); F(8)
-            ship("s", new, snd, 2, [new + "u1"]); ship("s", new, snd, 3, [new + "u1"])
-            fin(2)
-            ship("s", new, snd, 4, [new + "u2"]); ship("v", new, snd, 5, [new + "u2"])
-            exchange(k + 1, [snd + str(c) for c in range(6)])
-            if k == 0:
-                compare(1); compare(2)
-                fold(0, "X1")
-                op("v", ["lg"], ["lr0"], lambda: V.tensor_scalar(T.lr[:, 0:42], T.lg[:, 0:42], 1.0, None, Op.add))
-                op("v", ["lr0", "spotF"], ["lr0"], lambda: V.tensor_tensor(T.lr[:, 0:42], T.lr[:, 0:42], T.spotF[:, 0:42], Op.mult))
-                op("v", ["lr0", "strR"], ["lr1"], lambda: V.tensor_tensor(T.lr[:, 42:84], T.lr[:, 0:42], T.strR[:, 0:42], Op.add))
-                place(0, "X1", 0)
-                op("v", ["lr0", "lr1"], ["offR"], lambda: V.tensor_copy(T.offR[:], T.lr[:]))
-                place(0, "X1", 1)
-                place(0, "X1", 2)
-            low_init()
-            G(2); G(1); G(0)
+                op("v", ["#J", "rq%d" % k], ["#J"], lambda: V.tensor_tensor(dg, dg, T.rq[:, k * R:(k + 1) * R], Op.mult))
+                return
+            out, res = (T.Rw[:, 0:R], "r2") if k == 0 else (T.r3[:], "r3")
+            op("v", ["#J", "rr%d" % k], [res], lambda: V.tensor_tensor(out, T.rr[:, k * R:(k + 1) * R], dg, Op.subtract))
             if k == 1:
-                r_of_lower(0); r_of_lower(1)
-            F(0); F(1); M(2); F(2); M(1); fin3(); M(0); newton(0); fin2(); newton(1); fin01()
-            if k == 0:
-                pick("s", T.Rw[:, R:2 * R], T.sndR[:, 1:2 * R:2], ["r2"], "sndR1")
-                small("R", "sndR", "Rw", 2 * R, 2 * H, ["sndR0", "sndR1"])
-                op("s", ["r2"], ["rq1"], lambda: S.activation(T.rq[:, R:2 * R], T.Rw[:, R:2 * R], Act.Square))
-                op("s", ["r2"], ["rr1"], lambda: S.activation(T.rr[:, R:2 * R], T.Rw[:, R:2 * R], Act.Identity, scale=2.0))
-            else:
-                dma("q", "st", 0, T.inv[:], T.r3[:], ["r3"], [])
-                stores[0] += 16
-        else:
-            low_init()
-            init_up(0); init_up(1)
-            G(2); G(1); G(0)
-            for v in range(3, 9):
-                G(v)
-            F(0); F(1); M(2); F(2); M(1); F(3); M(0); M(3); fin3()
-            init_up(2)
-            F(4); M(4); fin2(); F(5); M(5); fin01()
-            store("q", 0, 4 * R, ["Yl0", "Yl2", "Yl3"])
-            M(6); fin(0); M(7); F(6); M(8); fin(1); F(7); F(8); fin_last(0); fin_last(1)
+                store("q", T.inv[:], T.r3[:], ["r3"])
 
-    stores = [0]
+        def weigh():
+            banks = ["#%s0" % xn, "#%s1" % xn]
+            out, res = (T[xn][:, 4:46, :], banks) if k == 1 else (T.Y[:, 0:3 * R], ["Yl"])
+            op("v", banks + ["rg%d" % k], res, lambda: V.tensor_tensor(out, T[xn][:, 4:46, :], T.rg[:, (k - 1) * 3 * R:k * 3 * R], Op.mult))
+
+        def r_round():
+            pick("s", T.Rw[:, 0:R], T.sndR[:], ["r2"], "sndR")
+            exchange("R", ["sndR"])
+            op("s", ["r2"], ["rq1"], lambda: S.activation(T.rq[:, R:2 * R], T.Rw[:, 0:R], Act.Square))
+            op("s", ["r2"], ["rr1"], lambda: S.activation(T.rr[:, R:2 * R], T.Rw[:, 0:R], Act.Identity, scale=2.0))
+
+        left = {"#B0": 4, "#B1": 4, "#B2": 4, "#%s0" % xn: 2 if merged else 4, "#%s1" % xn: 2, "#J": 2}
+        for word in ORDER[k].split():
+            c, a = word[0], word[1:]
+            n = int(a) if a.isdigit() else None
+            if c in "GH":
+                gather(n, 2 + (c == "H"))
+            elif c in "MN":
+                times(n, 2 + (c == "N"))
+            elif c == "F":
+                fused(n)
+            elif c == "f":
+                fin(n, 0, 2, "q")
+            elif c == "z":
+                fin(2, n, n + 1, "qs"[n])
+            elif c in "xX":
+                lo, hi = CHUNKS[n]
+                made = [new + "u%d" % i for i in range(lo // 2, hi // 2)]
+                exchange("%d%d" % (k + 1, n), ship("s" if c == "x" else "sv", new, snd, lo, hi, made))
+            elif word == "iL":
+                init_low()
+            elif c == "i":
+                init_up(int(a[1]))
+            elif c == "e":
+                compare(n)
+            elif c == "l":
+                if n == 0:
+                    start("J", 3)
+                fold(*groups[n])
+            elif c in "ab":
+                place(*groups[n], c == "b")
+            elif c == "m":
+                op("v", ["#%s0" % xn, "P0", "P1"], ["#%s0" % xn], lambda: V.tensor_tensor(
+                    T[xn][:, 4:32, :], T[xn][:, 4:32, :], T.G[:, 0:2, 2 * R:3 * R], Op.subtract))
+            elif word == "c2":
+                copy("s", T.x2[:, k * R:(k + 1) * R], T[xn][:, 32:46, :], ["#%s1" % xn], ["x2%d" % k])
+            elif c == "d":
+                diagonal()
+            elif c == "n":
+                newton(n)
+            elif c == "w":
+                weigh()
+            elif c == "y":
+                store("q", T.y[:, 0:4 * R], T.Y[:, 0:4 * R], ["Yl", "Yd"])
+            elif word == "rA":
+                op("s", ["Dw", "haloD", "spotU"], ["rg1"], lambda: S.activation(
+                    T.rg[:, 0:3 * R], T.Dw[:, 0:2 * R].indirect(T.spotU[:, 0:42]), Act.Identity, bias=2.0, scale=-1.0))
+            elif word == "rB":
+                copy("s", T.rg[:, 3 * R:6 * R], T.Rw[:, 0:2 * R].indirect(T.spotU[:, 0:42]), ["r2", "haloR", "spotU"], ["rg2"])
+            else:
+                r_round()
+
     for k in range(3):
         sweep(k)
     for sem, n in count.items():

@@ -10,19 +10,26 @@ LIFT = 64
 F32, BF, I32, U16 = "float32", "bfloat16", "int32", "uint16"
 
 SCRATCH = {
-    "shipI": ("sbuf", [128, NB, 2], I32), "shipU": ("sbuf", [128, 14], U16), "shipW": ("sbuf", [128, NB, 6, 2], I32),
-    "ship2": ("sbuf", [128, 28], U16), "ship4": ("sbuf", [128, 56], U16), "ship6": ("sbuf", [128, 84], U16),
-    "spotI": ("sbuf", [128, 126], I32), "spotU": ("sbuf", [128, 42], U16), "spotF": ("sbuf", [128, 126], F32),
-    "hi": ("sbuf", [128, 126], I32), "lg": ("sbuf", [128, 126], F32), "stride": ("sbuf", [128, 126], F32),
-    "nbo": ("sbuf", [128, 126], F32), "d1": ("sbuf", [128, 126], F32), "d2": ("sbuf", [128, 126], F32),
+    "shipI": ("sbuf", [128, NB, 2], I32), "shipU": ("sbuf", [128, 14], U16), "shipB": ("sbuf", [128, NB, 2], BF),
+    "ship2": ("sbuf", [128, 28], U16), "ship6": ("sbuf", [128, 84], U16), "ioS": ("sbuf", [128, NB, 12], BF),
+    "spotI": ("sbuf", [128, 42], I32), "spotU": ("sbuf", [128, 42], U16),
+    "ioP": ("sbuf", [128, 1], I32), "pmI": ("sbuf", [128, 1], I32), "pmF": ("sbuf", [128, 1], F32),
+    "tab": ("sbuf", [128, 14, 3], F32), "Wf": ("sbuf", [128, 320], F32),
+    "idP": ("sbuf", [128, 128], BF), "idM": ("sbuf", [128, 128], BF),
+    "key": ("sbuf", [128, 14, 3, 3], F32), "tmp": ("sbuf", [128, 3, 14, 3], F32), "srt": ("sbuf", [128, 3, 14, 3], F32),
+    "srtI": ("sbuf", [128, 3, 14, 2], I32), "low": ("sbuf", [128, 3, 14, 2], I32), "less": ("sbuf", [128, 14, 3], BF),
+    "fromU": ("sbuf", [128, 42], U16), "backU": ("sbuf", [128, 42], U16),
+    "lowS": ("sbuf", [128, 3 * R], BF), "Ys": ("sbuf", [128, 3 * R], F32),
+    "hi": ("sbuf", [128, 42], I32), "lg": ("sbuf", [128, 42], F32), "Z": ("sbuf", [128, 2, 252], F32),
+    "nbo": ("sbuf", [128, 42], F32), "d1": ("sbuf", [128, 42], F32), "d2": ("sbuf", [128, 42], F32),
     "jt": ("sbuf", [128, 378], F32), "off": ("sbuf", [128, 378], U16),
     "colI": ("sbuf", [128, R], I32), "colF": ("sbuf", [128, 2 * R], F32), "sndC": ("sbuf", [128, R], F32),
     "colT": ("sbuf", [128, 14, 16], F32), "repU": ("sbuf", [128, 42, 7, 6], F32),
-    "rep0": ("sbuf", [128, 14, 3, 6], F32), "repL": ("sbuf", [128, 42, 2, 6], F32),
+    "repL": ("sbuf", [128, 42, 6], F32),
     "cug": ("sbuf", [128, 3 * R], F32), "eq": ("sbuf", [128, 9 * 252], BF),
-    "ioJ": ("sbuf", [128, 128], BF), "ioK": ("sbuf", [128, 128], BF),
+    "ioJ": ("sbuf", [128, 160], BF), "ioK": ("sbuf", [128, 128], BF),
     "idB": ("sbuf", [128, 128], BF), "idN": ("sbuf", [128, 128], F32),
-    "W0": ("sbuf", [128, 512], BF), "W": ("sbuf", [128, 6 * 512], BF),
+    "W0": ("sbuf", [128, 320], BF), "W": ("sbuf", [128, 6 * 320], BF),
     "lowd": ("sbuf", [128, 4 * R], BF), "A": ("sbuf", [128, WIN], BF),
     "U1": ("sbuf", [128, WIN], F32), "U2": ("sbuf", [128, WIN], F32),
     "sndA": ("sbuf", [128, NB * BLK], BF), "snd1": ("sbuf", [128, NB * BLK], F32), "snd2": ("sbuf", [128, NB * BLK], F32),
@@ -30,7 +37,7 @@ SCRATCH = {
     "relC": ("sbuf", [128, H], F32), "relD": ("sbuf", [128, H], BF), "relR": ("sbuf", [128, H], F32),
     "Dw": ("sbuf", [128, 2 * R], BF), "sndD": ("sbuf", [128, R], BF),
     "Rw": ("sbuf", [128, 2 * R], F32), "sndR": ("sbuf", [128, R], F32),
-    "G": ("sbuf", [128, 9, 3 * R], F32), "x2": ("sbuf", [128, 2 * R], F32), "rg": ("sbuf", [128, 6 * R], F32),
+    "G": ("sbuf", [128, 9, 3 * R], F32), "x2": ("sbuf", [128, R], F32), "rg": ("sbuf", [128, 6 * R], F32),
     "rq": ("sbuf", [128, 2 * R], F32), "rr": ("sbuf", [128, 2 * R], F32), "r3": ("sbuf", [128, R], F32),
     "Y": ("sbuf", [128, 10 * R], F32),
     "XA": ("psum", [128, 64, 16], F32), "XB": ("psum", [128, 64, 16], F32), "J": ("psum", [128, 512], F32),
@@ -45,16 +52,26 @@ for _k in (1, 2):
 DIRECT = "CDR"
 SHARE = ((0, 2), (2, 4), (0, 4))
 RELAYED = [n for n in SENDS if n not in DIRECT]
+WAYS = "sssssss"
+FIVE = [n for n, w in zip(RELAYED, WAYS) if w == "f"]
+HAND = [n for n, w in zip(RELAYED, WAYS) if w == "h"]
 SEMAPHORES = ["cv", "cs", "cp", "cg", "lship", "lspot", "lcol", "lup", "llow", "ldg", "st",
               "arC", "arA", "ar1", "ar2", "arD", "arR", "sent"] + ["h" + n for n in RELAYED]
 
+LINES = "34567812"
+GROUPS = {3: ((3, 4), "J"), 5: ((5, 6, 7, 8), "B1"), 1: ((1, 2), "J")}
+ACUT = 26
+PREPARE = ""
+
 ORDER = (
-    "e4 e3 e5 e2 l3 e6 l5 e7 a3 e8 b3 l7 G3 G4 e0 a5 F3 e1 b5 H5 iB1 l0 M3 a7 M4 b7 F4 G6 G7 a0 G8 N5 b0 f0 iB2 x0 M6 H1 "
-    "M7 F6 M8 f1 iL x1 F8 F7 N1 G2 f2 X2 M2 G0 iB1 F2 M0 d n0 c2 iB0 n1 F0 iB2 m rA r",
-    "G3 iL F5 G4 F3 M3 G5 F6 G6 M4 F4 M5 M6 f0 G7 F7 G8 M7 M8 x0 f1 F8 F2 G1 M1 iB0 x1 f2 G2 G0 X2 "
-    "rB M2 F1 M0 iB1 F0 d n0 m w c2 n1 iB2",
-    "G0 iL G1 G2 G3 F0 F1 H4 M0 F2 H5 M1 G6 F3 M2 M3 G8 w N4 d N5 F6 G7 M6 M8 y f0 M7 f1 F7 F8 z0 z1",
+    ".iB .zz .WW .pm .sU .W1s .sB .W5s .W0s .pn .iN .Wfs .xC .cF .W3s .s6 .As .cT .po .KK .Av .kb .ka .W4s .s2 .o1 .o2 .o3 .r0 .W2v .ki .bk .r1s .kl .hi .pU .d2 .lg .B0 .xA .g2s .g1s .d1 .nbv .tdv .t1 .g0v .r2s .t2 .T0 .t3 .T1 .Z2s .Z3s .Z5s .T2 .rL .Z4s .fU .go3 .go5 e3 e4 e5 .fG e8 l3 e6 e7 l5 a3 .XA .go1 e0 b3 e2 .rM e1 G3 G4 F4 l1 a5 b5 .xD G5 G6 M3 F7 M4 iB2 iB1 G7 a1 G8 F3 M5 b1 F5 f0 M6 M7 F6 x0 M8 G2 iL f1 F8 X1 M2 f2 G1 X2 F2 F1 iB2 .rq rA n0 n1 r q iB1 iB0 M1 c3",
+    "F5 F3 G3 G4 iL G5 M3 F6 G6 M4 F4 M5 G7 G8 M6 f0 x0 M7 F7 M8 f1 G1 F8 iB1 .cm x1 F2 .iPs f2 X2 G2 .bP M1 M2 F1 n0 .bU n1 w iB2 iB0",
+    "rB G4 G1 G2 iL F1 F2 G3 M4 M1 F3 M2 G5 F5 M3 G6 G8 w G7 M5 u M6 D F6 y F4 M8 M7 f0 f1 F7 F8 z0 z1",
 )
+
+
+def share(name):
+    return ((0, 2), (2, 3), (3, 4)) if WAYS[RELAYED.index(name)] == "o" else SHARE
 
 
 def bits(engines):
@@ -95,11 +112,12 @@ def helper_program(g, core, T, topo, p, i, q):
     dst = T.cores[q]
     rid, pid = topo.addr(dst, core)
     n = len(topo.engines(core, dst))
-    for name in RELAYED:
+    mine = [name for name in RELAYED if i < 2 or name not in FIVE]
+    for name in mine:
         a, b = SENDS[name][3:]
-        g.wait_ge(T.sem["h" + name], (SHARE[i][1] - SHARE[i][0]) * n // 4)
+        g.wait_ge(T.sem["h" + name], (share(name)[i][1] - share(name)[i][0]) * n // 4)
         g.remote_dma(landing(T, name, p, q), T["rel" + name[0]][:, a:b], T.sem["ar" + name[0]], T.sem.sent, pid, rid, topo.mask(core, dst))
-    g.wait_ge(T.sem.sent, n * len(RELAYED))
+    g.wait_ge(T.sem.sent, n * len(mine))
 
 
 def rank_program(g, core, T, topo):
@@ -179,11 +197,16 @@ def rank_program(g, core, T, topo):
         jobs = [(off_chip[i * d:(i + 1) * d], cores[q], "ar" + kind, piece(q), landing(T, name, rank, q)) for i, q in enumerate(to)]
         got = d * len(to)
         if name not in DIRECT:
-            jobs += [(on_chip[lo * h:hi * h], c, "h" + name, piece(q), T["rel" + kind][:, a:b]) for (lo, hi), (c, q) in zip(SHARE, relay)]
+            jobs += [(on_chip[lo * h:hi * h], c, "h" + name, piece(q), T["rel" + kind][:, a:b]) for (lo, hi), (c, q) in zip(share(name), relay)]
             got += ne * len(relay)
+            if name in HAND:
+                jobs = jobs[4:6] + [(off_chip,) + jobs[6][1:]] + jobs[:4]
+            if name in FIVE:
+                q = relay[2][1]
+                jobs[-1] = (off_chip, cores[q], "ar" + kind, piece(q), landing(T, name, rank, q))
         while jobs:
             call, busy = [], []
-            while jobs and not set(jobs[0][0]) & set(busy):
+            while jobs and not set(jobs[0][0]) & set(busy) and len(busy) < 2 * ne:
                 es, c, sem, src, dst = jobs.pop(0)
                 busy += es
                 call.append(RemoteDMATransfer(dst_ids=[dst_id(c)], dma_engine_mask=bits(es), remote_sem=T.sem[sem], src=src, dst=dst))
@@ -192,8 +215,11 @@ def rank_program(g, core, T, topo):
         landed[kind] = landed.get(kind, 0) + got
         wr["halo" + kind] = ("ar" + kind, landed[kind])
 
-    def scaled(out, src, mul, add):
-        op("v", [src], [out], lambda: V.tensor_scalar(T[out][:], T[src][:], float(mul), float(add), Op.mult, Op.add))
+    def scaled(q, out, src, mul, add, read, res):
+        if q == "s":
+            op("s", [read], [res], lambda: S.activation(out, src, Act.Identity, bias=float(add), scale=float(mul)))
+        else:
+            op("v", [read], [res], lambda: V.tensor_scalar(out, src, float(mul), float(add), Op.mult, Op.add))
 
     def copy(q, out, src, reads, writes, chain=False):
         op(q, reads, writes, (lambda: V.tensor_copy(out, src)) if q == "v" else (lambda: S.activation(out, src, Act.Copy)), chain)
@@ -211,126 +237,237 @@ def rank_program(g, core, T, topo):
 
     op("v", [], ["colI"], lambda: V.memset(T.colI[:], 0))
     dma("q", "lship", 16, T.shipI[:], T.ship[:], [], ["shipI"])
-    dma("s", "lspot", 48, T.spotI[:, 0:42], T.spot[:], [], [])
+    dma("s", "lspot", 16, T.spotI[:], T.spot[:], [], ["spotI"])
     order("q", ["colI"], [])
     order("s", ["colI"], [])
     for k in range(8):
         dma("sq"[k % 2], "lcol", 128, T.colI[16 * k:16 * k + 10, :], T.col[k, :], [], [])
     wr["colI"] = ("lcol", 128)
     dma("s", "lup", 16, T.A[:, OWN:WIN], T.val[:, 4 * R:10 * R], [], ["Aup"])
-    for v in (1, 2):
-        dma("q", "lspot", 48, T.spotI[:, 42 * v:42 * v + 42], T.spot[:], [], ["spotI"] if v == 2 else [])
     dma("q", "ldg", 16, T.Dw[:, 0:R], T.val[:, 3 * R:4 * R], [], ["Dw"])
     dma("q", "llow", 16, T.lowd[:], T.val[:, 0:4 * R], [], ["lowd"])
-    op("g", [], ["ioJ"], lambda: g.iota(T.ioJ[:], [[-32, 4], [128, 2], [-1, 16]], 0, 1, allow_small_or_imprecise_dtypes=True))
     op("g", [], ["ioK"], lambda: g.iota(T.ioK[:], [[-1, 128]], 0, 1, allow_small_or_imprecise_dtypes=True))
-    for win in ("A", "U1", "U2"):
-        op("v", [], [win + "z"], lambda: V.memset(T[win][:, 0:HALO], 0.0))
-    for h in range(2):
-        for e in range(2):
-            lo = (2 * h + e) * 128
-            op("v", ["ioJ"], ["W0"], lambda: V.tensor_scalar(T.W0[:, lo:lo + 128], T.ioJ[:], float(16 * h + 128 * e), None, Op.is_equal), True)
-    op("v", ["ioK"], ["idB"], lambda: V.tensor_scalar(T.idB[:], T.ioK[:], 0.0, None, Op.is_equal))
-    op("v", ["ioK"], ["idN"], lambda: V.tensor_scalar(T.idN[:], T.ioK[:], 0.0, -1.0, Op.is_equal, Op.mult))
-    for w, q in enumerate("vvsvss"):
-        out = T.W[:, 512 * w:512 * w + 512]
-        if q == "s":
-            op("s", ["W0"], ["W%d" % w], lambda: S.activation(out, T.W0[:], Act.Identity, scale=float(LIFT + w)))
-        else:
-            op("v", ["W0"], ["W%d" % w], lambda: V.tensor_scalar(out, T.W0[:], float(LIFT + w), None, Op.mult))
+    op("g", [], ["ioS"], lambda: g.iota(T.ioS[:], [[0, NB], [R, 6], [0, 2]], 0, 0, allow_small_or_imprecise_dtypes=True))
+    op("g", [], ["ioJ"], lambda: g.iota(T.ioJ[:], [[-32, 5], [160, 2], [-1, 16]], -160, 1, allow_small_or_imprecise_dtypes=True))
+    op("g", [], ["ioP"], lambda: g.iota(T.ioP[:], [[0, 1]], 0, 1))
+    op("g", [], ["tab"], lambda: g.iota(T.tab[:], [[16, 14], [R, 3]], 0, 0, allow_small_or_imprecise_dtypes=True))
+    diag = T.lowd[:, 3 * R:4 * R]
 
-    copy("v", T.shipU[:], T.shipI[:], ["shipI"], ["shipU"])
-    for w in range(3):
-        op("v", ["shipI"], ["shipW"], lambda: V.tensor_scalar(T.shipW[:, :, w, :], T.shipI[:], float(w * R), None, Op.add), True)
-    pick("v", T.colI[:, 0:R], T.sndC[:], ["colI"], "sndC")
-    exchange("C", ["sndC"])
-    op("v", ["shipW"], ["shipX"], lambda: V.tensor_scalar(T.shipW[:, :, 3:6, :], T.shipW[:, :, 0:3, :], float(3 * R), None, Op.add))
-    copy("v", T.colF[:, 0:R], T.colI[:], ["colI"], ["colF"])
-    copy("v", T.ship6[:], T.shipW[:], ["shipW", "shipX"], ["ship6"])
-    op("v", ["colF"], ["colT"], lambda: V.transpose(T.colT[:], T.colF[:, 0:R]))
-    exchange("A", ship("vs", "A", "sndA", 0, 6, ["Aup"]))
-    for n in sorted(set(b - a for a, b in CHUNKS) - {6}):
-        copy("v", T["ship%d" % n][:], T.shipW[:, :, 0:n, :], ["shipW", "shipX"], ["ship%d" % n])
+    def half(h, e):
+        return slice(160 * h + 16 * (1 - e), 160 * h + 16 * (1 - e) + 128)
 
-    copy("v", T.spotU[:], T.spotI[:, 0:42], ["spotI"], ["spotU"])
-    copy("v", T.spotF[:], T.spotI[:], ["spotI"], ["spotF"])
-    op("v", ["spotI"], ["hi"], lambda: V.tensor_scalar(T.hi[:], T.spotI[:], 512 - H, None, Op.bitwise_and))
-    op("v", ["spotF"], ["lg"], lambda: V.tensor_scalar(T.lg[:], T.spotF[:], float(R), None, Op.is_ge))
-    scaled("d2", "spotF", 1.0 / R - 1.0 / H, 0.0)
-    scaled("d1", "hi", -5.0 / H, (6 * R - HALO - 0.25) / H + (OWN + 0.25) / R)
-    scaled("nbo", "spotF", -1.0 / R, LIFT - (OWN + 0.25) / R)
-    op("v", ["d1", "d2"], ["d1"], lambda: V.tensor_tensor(T.d1[:], T.d1[:], T.d2[:], Op.add))
-    scaled("stride", "lg", H - R, R)
-    op("v", ["d1", "lg"], ["d1"], lambda: V.tensor_tensor(T.d1[:], T.d1[:], T.lg[:], Op.mult))
-    for w in range(6):
-        copy("s", T.repU[:, 0:14, :, w], T.colT[:, :, 3:10], ["colT"], ["repU0"], True)
-    copy("s", T.repU[:, 14:28, :, :], T.repU[:, 0:14, :, :], ["repU0"], ["repU1"])
-    copy("v", T.repU[:, 28:42, :, :], T.repU[:, 0:14, :, :], ["repU0"], ["repU2"])
-    pick("s", T.Dw[:, 0:R], T.sndD[:], ["Dw"], "sndD")
-    exchange("D", ["sndD"])
+    def pair(out, a, b, alu, reads, res):
+        op("v", reads, [res], lambda: V.tensor_tensor(out, a, b, alu), True)
 
-    def init(bank, out, src, res):
-        op("p", [res, "idB"], [bank], lambda: P.matmul(out, T.idB[:], src, True, False))
+    def init(bank, out, src, res, stop=False):
+        op("p", [res, "idB"], [bank], lambda: P.matmul(out, T.idB[:], src, True, stop), True)
 
     def init_up(i):
         init("#B%d" % i, T["B%d" % i][:, 0:2 * R], T.A[:, OWN + 2 * i * R:OWN + (2 * i + 2) * R], "Aup")
 
-    def start(bank, n):
-        op("p", ["nbo", "idN"], ["#" + bank], lambda: P.matmul(T[bank][:, 0:42 * n], T.idN[:], T.nbo[:, 0:42 * n], True, False))
-        op("p", ["d1"], ["#" + bank], lambda: P.matmul(T[bank][:, 0:42 * n], T.idN[:], T.d1[:, 0:42 * n], False, False), True)
+    def start(v0):
+        bank, n, z, res = group(v0)
+        op("p", res + ["idN"], ["#" + bank], lambda: P.matmul(T[bank][:, 0:n], T.idN[:], T.Z[:, 0, z:z + n], True, False), True)
 
-    op("p", ["lowd", "idB"], ["#XA0"], lambda: P.matmul(T.XA[:, 4:32, :], T.idB[:], T.lowd[:, 0:2 * R], True, True))
-    op("p", ["lowd", "idB"], ["#XA1"], lambda: P.matmul(T.XA[:, 32:46, :], T.idB[:], T.lowd[:, 2 * R:3 * R], True, True))
-    init_up(0)
-    for bank in ("J", "B1", "B2"):
-        start(bank, 2)
+    def group(v0):
+        lines, bank = GROUPS[v0]
+        n = 42 * len(lines)
+        z = 252 - n if 1 in lines else 0
+        return bank, n, z, ["Z0", "Z1", "Z2"] + ["Z3"] * (n > 84) + ["Z4", "Z5"] * (z > 0)
 
-    for t, q in enumerate("vss"):
-        copy(q, T.cug[:, t * R:(t + 1) * R], T.colF[:, 0:2 * R].indirect(T.spotU[:, 14 * t:14 * t + 14]),
-             ["colF", "haloC", "spotU"], ["cug%d" % t])
-    for t in range(3):
-        op("v", ["cug%d" % t], ["#XB0", "#XB1"], lambda: V.transpose(T.XB[:, 14 * t:14 * t + 14, :], T.cug[:, t * R:(t + 1) * R]), True)
-    diag = T.lowd[:, 3 * R:4 * R]
-    op("s", ["lowd"], ["rq0"], lambda: S.activation(T.rq[:, 0:R], diag, Act.Square, bias=2.0, scale=-1.0))
-    op("s", ["lowd"], ["rr0"], lambda: S.activation(T.rr[:, 0:R], diag, Act.Identity, bias=4.0, scale=-2.0))
-    for w in range(6):
-        copy("s", T.rep0[:, :, :, w], T.colT[:, :, 0:3], ["colT"], ["rep0"], True)
-    for t, s in enumerate((slice(1, 3), slice(0, 3, 2), slice(0, 2))):
-        copy("s", T.repL[:, 14 * t:14 * t + 14, :, :], T.rep0[:, :, s, :], ["rep0"], ["repL"], True)
+    def prepare(word):
+        c, q = word[:2], word[-1]
+        n = int(word[1]) if word[1].isdigit() else None
+        if c == "zz":
+            for win in ("A", "U1", "U2"):
+                op("v", [], [win + "z"], lambda: V.memset(T[win][:, 0:HALO], 0.0))
+        elif c == "pm":
+            op("v", ["ioP"], ["pmI"], lambda: V.tensor_scalar(T.pmI[:], T.ioP[:], 15, None, Op.bitwise_and))
+        elif c == "pn":
+            copy("v", T.pmF[:], T.pmI[:], ["pmI"], ["pmF"])
+        elif c == "po":
+            op("v", ["pmF", "tab"], ["tab"], lambda: V.tensor_scalar(T.tab[:], T.tab[:], T.pmF[:], None, Op.add))
+        elif c == "Wf":
+            scaled(q, T.Wf[:], T.W0[:], 1024, 0, "W", "Wf")
+        elif c == "iP":
+            scaled(q, T.idP[:], T.idB[:], R, 0, "idB", "idP")
+            scaled(q, T.idM[:], T.idB[:], -R, 0, "idB", "idM")
+        elif c == "KK":
+            for h in range(2):
+                for e in range(2):
+                    op("p", ["Wf", "colT"], ["#XA0"], lambda: P.matmul(T.XA[:, 8:15, 3 * h:3 * h + 3], T.Wf[:, half(h, e)], T.colT[:, e:14:2, 0:3], e == 0, e == 1), True)
+        elif c == "ka":
+            for s in range(3):
+                pair(T.key[:, :, 0, s], T.XA[:, 8:15, s:6:3], T.spotI[:, 14 * s:14 * s + 14], Op.add, ["#XA0", "spotI"], "key0")
+        elif c == "kb":
+            pair(T.key[:, :, 1, :], T.XA[:, 8:15, 0:6], T.tab[:], Op.add, ["#XA0", "tab"], "key1")
+            copy("v", T.key[:, :, 2, :], T.XA[:, 8:15, 0:6], ["#XA0"], ["key2"])
+        elif c == "o1":
+            pair(T.tmp[:, 0, :, :], T.key[:, :, :, 0], T.key[:, :, :, 1], Op.min, ["key0", "key1", "key2"], "tmp0")
+            pair(T.tmp[:, 1, :, :], T.key[:, :, :, 0], T.key[:, :, :, 1], Op.max, ["key0", "key1", "key2"], "tmp1")
+        elif c == "o2":
+            pair(T.tmp[:, 2, :, :], T.tmp[:, 0, :, :], T.key[:, :, :, 2], Op.max, ["tmp0"], "tmp2")
+            pair(T.srt[:, 2, :, :], T.tmp[:, 0, :, :], T.key[:, :, :, 2], Op.min, ["tmp0"], "srt2")
+        elif c == "o3":
+            pair(T.srt[:, 0, :, :], T.tmp[:, 1, :, :], T.tmp[:, 2, :, :], Op.max, ["tmp1", "tmp2"], "srt0")
+            pair(T.srt[:, 1, :, :], T.tmp[:, 1, :, :], T.tmp[:, 2, :, :], Op.min, ["tmp1", "tmp2"], "srt1")
+        elif c == "ki":
+            copy("v", T.srtI[:], T.srt[:, :, :, 0:2], ["srt0", "srt1", "srt2"], ["srtI"])
+        elif c == "kl":
+            op("v", ["srtI"], ["low"], lambda: V.tensor_scalar(T.low[:], T.srtI[:], 1023, None, Op.bitwise_and))
+        elif c == "fU":
+            copy("v", T.fromU[:], T.low[:, :, :, 1], ["low"], ["fromU"])
+        elif c == "fG":
+            copy("s", T.lowS[:], T.lowd[:, 0:3 * R].indirect(T.fromU[:, 0:42]), ["lowd", "fromU"], ["lowS"])
+        elif c == "bk":
+            for e in range(2):
+                for h in range(2):
+                    op("p", ["Wf", "srt0", "srt1"], ["#XA0"], lambda: P.matmul(T.XA[:, 16:18, e:14:2], T.Wf[:, half(e, h)], T.srt[:, 0:2, h:14:2, 2], h == 0, h == 1), True)
+        elif c == "cm":
+            pair(T.less[:, :, 0:2], T.key[:, :, 0, 0:2], T.key[:, :, 0, 1:3], Op.is_lt, ["key0"], "less")
+            pair(T.less[:, :, 2], T.key[:, :, 0, 0], T.key[:, :, 0, 2], Op.is_lt, ["key0"], "less")
+        elif c == "bP":
+            for s, terms in enumerate(((("idM", 0), ("idM", 2)), (("idP", 0), ("idM", 1)), (("idP", 2), ("idP", 1)))):
+                out = T.B0[:, 14 * s:14 * s + 14]
+                op("p", ["tab", "idN"], ["#B0"], lambda: P.matmul(out, T.idN[:], T.tab[:, :, s], True, False), True)
+                for i, (m, j) in enumerate(terms):
+                    op("p", ["less", m], ["#B0"], lambda: P.matmul(out, T[m][:], T.less[:, :, j], False, i == 1), True)
+        elif c == "bU":
+            scaled("v", T.backU[:], T.B0[:, 0:42], -1, 0, "#B0", "backU")
+        elif c == "B0":
+            init_up(0)
+        elif c == "iB":
+            op("v", ["ioK"], ["idB"], lambda: V.tensor_scalar(T.idB[:], T.ioK[:], 0.0, None, Op.is_equal))
+        elif c == "iN":
+            op("v", ["ioK"], ["idN"], lambda: V.tensor_scalar(T.idN[:], T.ioK[:], 0.0, -1.0, Op.is_equal, Op.mult))
+        elif c == "WW":
+            for h in range(2):
+                op("v", ["ioJ"], ["W"], lambda: V.tensor_scalar(T.W0[:, 160 * h:160 * h + 160], T.ioJ[:], float(16 * h), None, Op.is_equal), True)
+        elif c[0] == "W":
+            scaled(q, T.W[:, 320 * n:320 * n + 320], T.W0[:], LIFT + n, 0, "W", c)
+        elif c == "sU":
+            copy("v", T.shipU[:], T.shipI[:], ["shipI"], ["shipU"])
+        elif c == "sB":
+            copy("v", T.shipB[:], T.shipI[:], ["shipI"], ["shipB"])
+            init("#XB0", T.XB[:, 0:NB, 0:12], T.ioS[:], "ioS")
+            for w in range(6):
+                op("p", ["shipB"], ["#XB0"], lambda: P.matmul(T.XB[:, 0:NB, 2 * w:2 * w + 2], T.idB[:], T.shipB[:], False, w == 5), True)
+        elif c[0] == "s":
+            copy("v", T["ship%d" % n][:], T.XB[:, 0:NB, 0:2 * n], ["#XB0"], ["ship%d" % n])
+        elif c == "xC":
+            pick("v", T.colI[:, 0:R], T.sndC[:], ["colI"], "sndC")
+            exchange("C", ["sndC"])
+        elif c == "cF":
+            copy("v", T.colF[:, 0:R], T.colI[:], ["colI"], ["colF"])
+        elif c == "cT":
+            op("v", ["colF"], ["colT"], lambda: V.transpose(T.colT[:], T.colF[:, 0:R]))
+        elif c[0] == "A":
+            lo, hi = (0, ACUT) if q == "v" else (ACUT, 84)
+            copy(q, T.sndA[:, 16 * lo:16 * hi], T.A[:, OWN:WIN].indirect(T.ship6[:, lo:hi]), ["Aup", "ship6"], ["snd" + c])
+        elif c == "xA":
+            exchange("A", ["sndAv", "sndAs"])
+        elif c == "xD":
+            pick("s", T.Dw[:, 0:R], T.sndD[:], ["Dw"], "sndD")
+            exchange("D", ["sndD"])
+        elif c == "pU":
+            copy("v", T.spotU[:], T.low[:, :, :, 0], ["low"], ["spotU"])
+        elif c == "hi":
+            op("v", ["srtI"], ["hi"], lambda: V.tensor_scalar(T.hi[:], T.srtI[:, :, :, 0], 512 - H, None, Op.bitwise_and))
+        elif c == "lg":
+            op("v", ["hi"], ["lg"], lambda: V.tensor_scalar(T.lg[:], T.hi[:], float(R), None, Op.is_ge))
+        elif c == "d2":
+            scaled("v", T.d2[:], T.low[:, :, :, 0], 1.0 / R - 1.0 / H, 0.0, "low", "d2")
+        elif c == "d1":
+            scaled("v", T.d1[:], T.hi[:], -5.0 / H, (6 * R - HALO - 0.25) / H + (OWN + 0.25) / R, "hi", "d1")
+        elif c == "nb":
+            if q == "s":
+                scaled("s", T.nbo[:], T.d2[:], 1.0 / 6, LIFT - (OWN + 0.25) / R, "d2", "nbo")
+            else:
+                scaled("v", T.nbo[:], T.low[:, :, :, 0], -1.0 / R, LIFT - (OWN + 0.25) / R, "low", "nbo")
+        elif c == "t1":
+            op("v", ["d1", "d2"], ["d1"], lambda: V.tensor_tensor(T.d1[:], T.d1[:], T.d2[:], Op.add))
+        elif c == "td":
+            scaled(q, T.Z[:, 1, 0:42], T.lg[:], H - R, R, "lg", "Z1")
+        elif c == "t3":
+            op("v", ["d1", "nbo"], ["Z0"], lambda: V.tensor_tensor(T.Z[:, 0, 0:42], T.d1[:], T.nbo[:], Op.add))
+        elif c[0] == "Z":
+            lo, a, b = ((42, 0, 42), (84, 0, 84), (168, 28, 42), (182, 14, 84))[n - 2]
+            copy(q, T.Z[:, :, lo:lo + b - a], T.Z[:, :, a:b], ["Z0", "Z1"] + ["Z2"] * (b > 42), [c])
+        elif c == "t2":
+            op("v", ["d1", "lg"], ["d1"], lambda: V.tensor_tensor(T.d1[:], T.d1[:], T.lg[:], Op.mult))
+        elif c == "r0":
+            for w in range(6):
+                copy("s", T.repU[:, 0:14, :, w], T.colT[:, :, 3:10], ["colT"], ["repU0"], True)
+        elif c == "rL":
+            for w in range(6):
+                op("s", ["#XA0"], ["repL"], lambda: S.activation(T.repL[:, 14:42, w], T.XA[:, 16:18, 0:14], Act.Identity, scale=2.0 ** -20), True)
+        elif c == "rM":
+            copy("s", T.repL[:, 0:14, :], T.repL[:, 14:28, :], ["repL"], ["repM"])
+        elif c == "rq":
+            op("s", ["lowd"], ["rq0"], lambda: S.activation(T.rq[:, 0:R], diag, Act.Square, bias=2.0, scale=-1.0))
+            op("s", ["lowd"], ["rr0"], lambda: S.activation(T.rr[:, 0:R], diag, Act.Identity, bias=4.0, scale=-2.0))
+        elif c[0] == "r":
+            out, src = T.repU[:, 14 * n:14 * n + 14, :, :], T.repU[:, 0:14, :, :]
+            if q == "q":
+                dma("q", "lrep%d" % n, 16, out, src, ["repU0"], ["repU%d" % n])
+            else:
+                copy(q, out, src, ["repU0"], ["repU%d" % n])
+        elif c == "XA":
+            init("#XA0", T.XA[:, 4:32, :], T.lowS[:, 0:2 * R], "lowS", True)
+            init("#XA1", T.XA[:, 32:46, :], T.lowS[:, 2 * R:3 * R], "lowS", True)
+        elif c == "go":
+            start(n or int(q))
+        elif c[0] == "g":
+            copy(q, T.cug[:, n * R:(n + 1) * R], T.colF[:, 0:2 * R].indirect(T.spotU[:, 14 * n:14 * n + 14]),
+                 ["colF", "haloC", "spotU"], ["cug%d" % n])
+        else:
+            op("v", ["cug%d" % n], ["#XB0", "#XB1"], lambda: V.transpose(T.XB[:, 14 * n:14 * n + 14, :], T.cug[:, n * R:(n + 1) * R]), n > 0)
+
+    for word in PREPARE.split():
+        prepare(word)
 
     def compare(v):
-        rep, res = (T.repL[:, :, v, :], ["repL"]) if v < 2 else (T.repU[:, :, v - 2, :], ["repU0", "repU1", "repU2"])
-        op("v", ["#XB0", "#XB1"] + res, ["eq%d" % v],
-           lambda: V.tensor_tensor(T.eq[:, 252 * v:252 * v + 252], T.XB[:, 0:42, 4:10], rep, Op.is_equal))
+        lo, n, cut, rep, res = 252 * LINES.find(str(v)), 252, T.XB[:, 0:42, 4:10], T.repU[:, :, v - 2, :], ["repU0", "repU1", "repU2"]
+        if v == 0:
+            lo, n, cut, rep, res = 6 * 252, 84, T.XB[:, 28:42, 4:10], T.repL[:, 28:42, :], ["repL"]
+        elif v == 1:
+            lo, n, cut, rep, res = 6 * 252 + 84, 168, T.XB[:, 14:42, 4:10], T.repL[:, 0:28, :], ["repL", "repM"]
+        op("v", ["#XB0", "#XB1"] + res, ["eq%d" % v], lambda: V.tensor_tensor(T.eq[:, lo:lo + n], cut, rep, Op.is_equal))
 
-    def fold(v0, n, bank):
+    def fold(v0):
+        bank, n, z, _ = group(v0)
+        lines, a = GROUPS[v0][0], 252 * LINES.find(str(v0))
         for h in range(2):
             for i in range(12):
                 w, e = i // 2, i % 2
-                lo = 512 * w + (2 * h + e) * 128
-                op("p", ["eq%d" % v for v in range(v0, v0 + n)] + ["W%d" % w], ["#" + bank],
-                   lambda: P.matmul(T[bank][:, h:42 * n:2], T.W[:, lo:lo + 128],
-                                    T.eq[:, 252 * v0 + 6 * e + w:252 * (v0 + n):12], False, h == 1 and i == 11), True)
+                lo = 320 * w + half(h, e).start
+                op("p", ["eq%d" % v for v in lines + (0,) * (z > 0)] + ["W%d" % w], ["#" + bank],
+                   lambda: P.matmul(T[bank][:, h:n:2], T.W[:, lo:lo + 128], T.eq[:, a + 6 * e + w:a + 6 * n:12], False, h == 1 and i == 11), True)
 
-    def place(v0, n, bank, step):
-        a, b = 42 * v0, 42 * (v0 + n)
+    def place(v0, step):
+        bank, n, z, res = group(v0)
+        a = 42 * LINES.find(str(v0))
         if step == 0:
-            op("v", ["#" + bank, "stride"], ["jt%d" % v0], lambda: V.tensor_tensor(T.jt[:, a:b], T[bank][:, 0:b - a], T.stride[:, 0:b - a], Op.mult))
+            op("v", ["#" + bank] + res, ["jt%d" % v0], lambda: V.tensor_tensor(T.jt[:, a:a + n], T[bank][:, 0:n], T.Z[:, 1, z:z + n], Op.mult))
         else:
-            copy("v", T.off[:, a:b], T.jt[:, a:b], ["jt%d" % v0], ["off%d" % v for v in range(v0, v0 + n)])
+            copy("v", T.off[:, a:a + n], T.jt[:, a:a + n], ["jt%d" % v0], ["off%d" % v for v in GROUPS[v0][0]])
 
-    groups = {3: (3, 2, "J"), 5: (5, 2, "B1"), 7: (7, 2, "B2"), 0: (0, 3, "J")}
+    def offsets(v, t, n):
+        a = 42 * LINES.find(str(v)) + 14 * t
+        return T.off[:, a:a + 14 * n]
 
     def sweep(k):
         win, new, snd = ("A", "U1", "U2")[k], ("U1", "U2", None)[k], ("snd1", "snd2", None)[k]
-        whole = [win + "z", "halo" + "A12"[k]] + (["Aup"] if k == 0 else [win + "u%d" % i for i in range(3)])
+        whole = [win + "z", "halo" + "A12"[k]]  + (["Aup"] if k == 0 else [win + "u%d" % i for i in range(3)])
         xo, xn = ("XA", "XB", "XA")[k], ("XB", "XA", "XB")[k]
-        x2, x2n = (T.lowd[:, 2 * R:3 * R], "lowd") if k == 0 else (T.x2[:, (k - 1) * R:k * R], "x2%d" % (k - 1))
-        dg, merged = T.J[:, 0:R], "m" in ORDER[k]
+        x2, x2n = (T.lowS[:, 2 * R:3 * R], "lowS") if k < 2 else (T.x2[:], "x2")
+        dg, words = T.J[:, 0:R], ORDER[k].split()
+        third = [1] + [2] * ("d" not in words) + [3 + 2 * i + j for i in range(3) for j in range(2) if "g%d" % i in words]
 
         def gather(v, n):
+            t = int(v == 1)
             op("s", whole + ["off%d" % v], ["G%d" % v] + ["P%d" % v] * (n - 2), lambda: S.activation(
-                T.G[:, v, 0:n * R], T[win][:, 0:WIN].indirect(T.off[:, 42 * v:42 * v + 14 * n]), Act.Copy))
+                T.G[:, v, t * R:(t + n) * R], T[win][:, 0:WIN].indirect(offsets(v, t, n)), Act.Copy))
 
         def target(v, t):
             if v >= 3:
@@ -338,8 +475,8 @@ def rank_program(g, core, T, topo):
                 return "#B%d" % i, T["B%d" % i][:, j * R:(j + 1) * R]
             if v == 2:
                 return "#J", dg
-            s = [s for s in range(3) if s != t][v]
-            return "#%s%d" % (xn, s // 2), T[xn][:, 4 + 14 * s:18 + 14 * s, :]
+            s = int(t == 0)
+            return "#%s0" % xn, T[xn][:, 4 + 14 * s:18 + 14 * s, :]
 
         def sub(v, t, res):
             bank, out = target(v, t)
@@ -347,16 +484,18 @@ def rank_program(g, core, T, topo):
             op("p", [res, "idN"], [bank], lambda: P.matmul(out, T.idN[:], T.G[:, v, t * R:(t + 1) * R], False, left[bank] == 0), True)
 
         def fused(v):
+            t = 2 * (v != 1)
             op("v", whole + ["off%d" % v, x2n], ["P%d" % v], lambda: V.tensor_tensor(
-                T.G[:, v, 2 * R:3 * R], T[win][:, 0:WIN].indirect(T.off[:, 42 * v + 28:42 * v + 42]), x2, Op.mult))
-            if v < 2 and not merged:
-                sub(v, 2, "P%d" % v)
+                T.G[:, v, t * R:(t + 1) * R], T[win][:, 0:WIN].indirect(offsets(v, t, 1)), x2, Op.mult))
+            if v in third:
+                sub(v, t, "P%d" % v)
 
         def times(v, n):
-            gv, res = T.G[:, v, 0:n * R], ["G%d" % v] + ["P%d" % v] * (n - 2)
-            op("v", res + ["#%s%d" % (xo, j) for j in range(n - 1)], res,
-               lambda: V.tensor_tensor(gv, gv, T[xo][:, 4:4 + 14 * n, :], Op.mult))
-            for t in range(n if v < 2 and not merged else 2):
+            t0 = int(v == 1)
+            gv, res = T.G[:, v, t0 * R:(t0 + n) * R], ["G%d" % v] + ["P%d" % v] * (n - 2)
+            op("v", res + ["#%s%d" % (xo, j) for j in range(t0 + n - 1)], res,
+               lambda: V.tensor_tensor(gv, gv, T[xo][:, 4 + 14 * t0:4 + 14 * (t0 + n), :], Op.mult))
+            for t in range(t0, t0 + (n if v in third else 2)):
                 sub(v, t, res[0])
 
         def store(q, out, src, res):
@@ -367,14 +506,17 @@ def rank_program(g, core, T, topo):
             lo, hi = (2 * i + j0) * R, (2 * i + j1) * R
             out = T[new][:, OWN + lo:OWN + hi] if new else T.Y[:, 4 * R + lo:4 * R + hi]
             res = (new + "u%d" % i) if new else "Y%d" % lo
-            op("v", ["#B%d" % i] + ["P%d" % (3 + 2 * i + j) for j in range(j0, j1)], [res], lambda: V.tensor_tensor(
-                out, T["B%d" % i][:, j0 * R:j1 * R], T.G[:, 3 + 2 * i + j0:3 + 2 * i + j1, 2 * R:3 * R], Op.subtract))
+            if 3 + 2 * i in third:
+                copy("s", out, T["B%d" % i][:, j0 * R:j1 * R], ["#B%d" % i], [res])
+            else:
+                op("v", ["#B%d" % i] + ["P%d" % (3 + 2 * i + j) for j in range(j0, j1)], [res], lambda: V.tensor_tensor(
+                    out, T["B%d" % i][:, j0 * R:j1 * R], T.G[:, 3 + 2 * i + j0:3 + 2 * i + j1, 2 * R:3 * R], Op.subtract))
             if not new:
                 store(q, T.y[:, 4 * R + lo:4 * R + hi], out, [res])
 
         def init_low():
-            init("#%s0" % xn, T[xn][:, 4:32, :], T.lowd[:, 0:2 * R], "lowd")
-            init("#%s1" % xn, T[xn][:, 32:46, :], T.lowd[:, 2 * R:3 * R], "lowd")
+            init("#%s0" % xn, T[xn][:, 4:32, :], T.lowS[:, 0:2 * R], "lowS")
+            init("#%s1" % xn, T[xn][:, 32:46, :], T.lowS[:, 2 * R:3 * R], "lowS", True)
             init("#J", dg, diag, "lowd")
 
         def diagonal():
@@ -392,26 +534,29 @@ def rank_program(g, core, T, topo):
 
         def weigh():
             banks = ["#%s0" % xn, "#%s1" % xn]
-            out, res = (T[xn][:, 4:46, :], banks) if k == 1 else (T.Y[:, 0:3 * R], ["Yl"])
+            out, res = (T[xn][:, 4:46, :], banks) if k == 1 else (T.Ys[:], ["Ys"])
             op("v", banks + ["rg%d" % k], res, lambda: V.tensor_tensor(out, T[xn][:, 4:46, :], T.rg[:, (k - 1) * 3 * R:k * 3 * R], Op.mult))
 
         def r_round():
             pick("s", T.Rw[:, 0:R], T.sndR[:], ["r2"], "sndR")
             exchange("R", ["sndR"])
-            op("s", ["r2"], ["rq1"], lambda: S.activation(T.rq[:, R:2 * R], T.Rw[:, 0:R], Act.Square))
-            op("s", ["r2"], ["rr1"], lambda: S.activation(T.rr[:, R:2 * R], T.Rw[:, 0:R], Act.Identity, scale=2.0))
 
-        left = {"#B0": 4, "#B1": 4, "#B2": 4, "#%s0" % xn: 2 if merged else 4, "#%s1" % xn: 2, "#J": 2}
-        for word in ORDER[k].split():
+        left = {}
+        for v in range(1, 9):
+            for t in range(3 if v in third else 2):
+                left[target(v, t)[0]] = left.get(target(v, t)[0], 0) + 1
+        for word in words:
             c, a = word[0], word[1:]
             n = int(a) if a.isdigit() else None
-            if c in "GH":
+            if c == ".":
+                prepare(a)
+            elif c in "GH":
                 gather(n, 2 + (c == "H"))
             elif c in "MN":
                 times(n, 2 + (c == "N"))
             elif c == "F":
                 fused(n)
-            elif c == "f":
+            elif c in "fg":
                 fin(n, 0, 2, "q")
             elif c == "z":
                 fin(2, n, n + 1, "qs"[n])
@@ -426,18 +571,22 @@ def rank_program(g, core, T, topo):
             elif c == "e":
                 compare(n)
             elif c == "l":
-                if n == 0:
-                    start("J", 3)
-                fold(*groups[n])
+                fold(n)
+            elif c == "q":
+                op("s", ["r2"], ["rq1"], lambda: S.activation(T.rq[:, R:2 * R], T.Rw[:, 0:R], Act.Square))
+                op("s", ["r2"], ["rr1"], lambda: S.activation(T.rr[:, R:2 * R], T.Rw[:, 0:R], Act.Identity, scale=2.0))
             elif c in "ab":
-                place(*groups[n], c == "b")
-            elif c == "m":
-                op("v", ["#%s0" % xn, "P0", "P1"], ["#%s0" % xn], lambda: V.tensor_tensor(
-                    T[xn][:, 4:32, :], T[xn][:, 4:32, :], T.G[:, 0:2, 2 * R:3 * R], Op.subtract))
+                place(n, c == "b")
+            elif c == "u":
+                copy("s", T.Y[:, 0:3 * R], T.Ys[:, 0:3 * R].indirect(T.backU[:, 0:42]), ["Ys", "backU"], ["Yl"])
             elif word == "c2":
-                copy("s", T.x2[:, k * R:(k + 1) * R], T[xn][:, 32:46, :], ["#%s1" % xn], ["x2%d" % k])
+                copy("s", T.x2[:], T[xn][:, 32:46, :], ["#%s1" % xn], ["x2"])
+            elif word == "c3":
+                op("v", ["lowS", "rg1"], ["x2"], lambda: V.tensor_tensor(T.x2[:], T.lowS[:, 2 * R:3 * R], T.rg[:, 2 * R:3 * R], Op.mult))
             elif c == "d":
                 diagonal()
+            elif c == "D":
+                copy("s", T.Y[:, 3 * R:4 * R], dg, ["#J"], ["Yd"])
             elif c == "n":
                 newton(n)
             elif c == "w":

from concourse.bass import DstId, RemoteDMATransfer
from concourse.mybir import AluOpType as Op, ActivationFunctionType as Act

R, H, NB = 224, 32, 7
BLK = 6 * H
HALO = 16
OWN = HALO + NB * BLK
WIN = OWN + 6 * R
LIFT = 64
F32, BF, I32, U16 = "float32", "bfloat16", "int32", "uint16"

SCRATCH = {
    "shipI": ("sbuf", [128, NB, 2], I32), "shipU": ("sbuf", [128, 14], U16), "shipB": ("sbuf", [128, NB, 2], BF),
    "ship2": ("sbuf", [128, 28], U16), "ship6": ("sbuf", [128, 84], U16), "ioS": ("sbuf", [128, NB, 12], BF),
    "spotI": ("sbuf", [128, 42], I32), "spotU": ("sbuf", [128, 42], U16),
    "ioP": ("sbuf", [128, 1], I32), "pmI": ("sbuf", [128, 1], I32), "pmF": ("sbuf", [128, 1], F32),
    "tab": ("sbuf", [128, 14, 3], F32), "Wf": ("sbuf", [128, 320], F32),
    "idP": ("sbuf", [128, 128], BF), "idM": ("sbuf", [128, 128], BF),
    "key": ("sbuf", [128, 14, 3, 3], F32), "tmp": ("sbuf", [128, 3, 14, 3], F32), "srt": ("sbuf", [128, 3, 14, 3], F32),
    "srtI": ("sbuf", [128, 3, 14, 2], I32), "low": ("sbuf", [128, 3, 14, 2], I32), "less": ("sbuf", [128, 14, 3], BF),
    "fromU": ("sbuf", [128, 42], U16), "backU": ("sbuf", [128, 42], U16),
    "lowS": ("sbuf", [128, 3 * R], BF), "Ys": ("sbuf", [128, 3 * R], F32),
    "hi": ("sbuf", [128, 42], I32), "lg": ("sbuf", [128, 42], F32), "Z": ("sbuf", [128, 2, 252], F32),
    "nbo": ("sbuf", [128, 42], F32), "d1": ("sbuf", [128, 42], F32), "d2": ("sbuf", [128, 42], F32),
    "jt": ("sbuf", [128, 378], F32), "off": ("sbuf", [128, 378], U16),
    "colI": ("sbuf", [128, R], I32), "colF": ("sbuf", [128, 2 * R], F32), "sndC": ("sbuf", [128, R], F32),
    "colT": ("sbuf", [128, 14, 16], F32), "repU": ("sbuf", [128, 42, 7, 6], F32),
    "repL": ("sbuf", [128, 42, 6], F32),
    "cug": ("sbuf", [128, 3 * R], F32), "eq": ("sbuf", [128, 9 * 252], BF),
    "ioJ": ("sbuf", [128, 160], BF), "ioK": ("sbuf", [128, 128], BF),
    "idB": ("sbuf", [128, 128], BF), "idN": ("sbuf", [128, 128], F32),
    "W0": ("sbuf", [128, 320], BF), "W": ("sbuf", [128, 6 * 320], BF),
    "lowd": ("sbuf", [128, 4 * R], BF), "A": ("sbuf", [128, WIN], BF),
    "U1": ("sbuf", [128, WIN], F32), "U2": ("sbuf", [128, WIN], F32),
    "sndA": ("sbuf", [128, NB * BLK], BF), "snd1": ("sbuf", [128, NB * BLK], F32), "snd2": ("sbuf", [128, NB * BLK], F32),
    "relA": ("sbuf", [128, BLK], BF), "rel1": ("sbuf", [128, BLK], F32), "rel2": ("sbuf", [128, BLK], F32),
    "relC": ("sbuf", [128, H], F32), "relD": ("sbuf", [128, H], BF), "relR": ("sbuf", [128, H], F32),
    "Dw": ("sbuf", [128, 2 * R], BF), "sndD": ("sbuf", [128, R], BF),
    "Rw": ("sbuf", [128, 2 * R], F32), "sndR": ("sbuf", [128, R], F32),
    "G": ("sbuf", [128, 9, 3 * R], F32), "x2": ("sbuf", [128, R], F32), "rg": ("sbuf", [128, 6 * R], F32),
    "rq": ("sbuf", [128, 2 * R], F32), "rr": ("sbuf", [128, 2 * R], F32), "r3": ("sbuf", [128, R], F32),
    "Y": ("sbuf", [128, 10 * R], F32),
    "XA": ("psum", [128, 64, 16], F32), "XB": ("psum", [128, 64, 16], F32), "J": ("psum", [128, 512], F32),
    "B0": ("psum", [128, 512], F32), "B1": ("psum", [128, 512], F32), "B2": ("psum", [128, 512], F32),
}
CHUNKS = ((0, 2), (2, 4), (4, 6))
SENDS = {"C": ("colF", R, H, 0, H), "A": ("A", HALO, BLK, 0, BLK), "D": ("Dw", R, H, 0, H)}
for _k in (1, 2):
    for _i, (_a, _b) in enumerate(CHUNKS):
        SENDS["%d%d" % (_k, _i)] = ("U%d" % _k, HALO, BLK, H * _a, H * _b)
    SENDS.setdefault("R", ("Rw", R, H, 0, H))
DIRECT = "CDR"
SHARE = ((0, 2), (2, 4), (0, 4))
RELAYED = [n for n in SENDS if n not in DIRECT]
WAYS = "sssssss"
FIVE = [n for n, w in zip(RELAYED, WAYS) if w == "f"]
HAND = [n for n, w in zip(RELAYED, WAYS) if w == "h"]
SEMAPHORES = ["cv", "cs", "cp", "cg", "lship", "lspot", "lcol", "lup", "llow", "ldg", "st",
              "arC", "arA", "ar1", "ar2", "arD", "arR", "sent"] + ["h" + n for n in RELAYED]

LINES = "34567812"
GROUPS = {3: ((3, 4), "J"), 5: ((5, 6, 7, 8), "B1"), 1: ((1, 2), "J")}
ACUT = 26
PREPARE = ""

ORDER = (
    ".iB .zz .WW .pm .sU .W1s .sB .W5s .W0s .pn .iN .Wfs .xC .cF .W3s .s6 .As .cT .po .KK .Av .kb .ka .W4s .s2 .o1 .o2 .o3 .r0 .W2v .ki .bk .r1s .kl .hi .pU .d2 .lg .B0 .xA .g2s .g1s .d1 .nbv .tdv .t1 .g0v .r2s .t2 .T0 .t3 .T1 .Z2s .Z3s .Z5s .T2 .rL .Z4s .fU .go3 .go5 e3 e4 e5 .fG e8 l3 e6 e7 l5 a3 .XA .go1 e0 b3 e2 .rM e1 G3 G4 F4 l1 a5 b5 .xD G5 G6 M3 F7 M4 iB2 iB1 G7 a1 G8 F3 M5 b1 F5 f0 M6 M7 F6 x0 M8 G2 iL f1 F8 X1 M2 f2 G1 X2 F2 F1 iB2 .rq rA n0 n1 r q iB1 iB0 M1 c3",
    "F5 F3 G3 G4 iL G5 M3 F6 G6 M4 F4 M5 G7 G8 M6 f0 x0 M7 F7 M8 f1 G1 F8 iB1 .cm x1 F2 .iPs f2 X2 G2 .bP M1 M2 F1 n0 .bU n1 w iB2 iB0",
    "rB G4 G1 G2 iL F1 F2 G3 M4 M1 F3 M2 G5 F5 M3 G6 G8 w G7 M5 u M6 D F6 y F4 M8 M7 f0 f1 F7 F8 z0 z1",
)


def share(name):
    return ((0, 2), (2, 3), (3, 4)) if WAYS[RELAYED.index(name)] == "o" else SHARE


def bits(engines):
    m = 0
    for e in engines:
        m |= 1 << e
    return m


def routes(T, topo):
    cores, n, plan = T.cores, len(T.cores), []
    for p, c in enumerate(cores):
        order = [(p + k) % n for k in range(1, n)]
        mate = [q for q in order if topo.mates(c, cores[q])]
        plane = [q for q in order if topo.same_plane(c, cores[q])]
        far = [q for q in order if q not in mate and q not in plane]
        free = [h for h in topo.cores_of(c) if topo.die(h) != topo.die(c)]
        relay = []
        for q in far[1:] + plane[:1]:
            h = [h for h in free if topo.may_write(h, cores[q])][0]
            free.remove(h)
            relay.append((h, q))
        plan.append((mate + far[:1] + plane[1:], relay))
    return plan


def other(p, q):
    return p if p < q else p - 1


def landing(T, name, p, q):
    win, lo, pitch, a, b = SENDS[name]
    lo += other(p, q) * pitch
    return T[win][:, lo + a:lo + b]


def helper_program(g, core, T, topo, p, i, q):
    dst = T.cores[q]
    rid, pid = topo.addr(dst, core)
    n = len(topo.engines(core, dst))
    mine = [name for name in RELAYED if i < 2 or name not in FIVE]
    for name in mine:
        a, b = SENDS[name][3:]
        g.wait_ge(T.sem["h" + name], (share(name)[i][1] - share(name)[i][0]) * n // 4)
        g.remote_dma(landing(T, name, p, q), T["rel" + name[0]][:, a:b], T.sem["ar" + name[0]], T.sem.sent, pid, rid, topo.mask(core, dst))
    g.wait_ge(T.sem.sent, n * len(mine))


def rank_program(g, core, T, topo):
    rank = T.rank_of(core)
    plan = routes(T, topo)
    if rank is None:
        for p, (_, relay) in enumerate(plan):
            for i, (h, q) in enumerate(relay):
                if h == core:
                    helper_program(g, core, T, topo, p, i, q)
        return
    cores = T.cores
    direct, relay = plan[rank]
    V, S, P, Q = g.vector, g.scalar, g.tensor, g.sync
    eng = {"v": V, "s": S, "p": P, "q": Q, "g": g}
    count = {"cv": 0, "cs": 0, "cp": 0, "cg": 0}
    seen = {k: {} for k in eng}
    wr, rd = {}, {}

    def need(q, tok):
        if seen[q].get(tok[0], 0) < tok[1]:
            seen[q][tok[0]] = tok[1]
            eng[q].wait_ge(T.sem[tok[0]], tok[1])

    def order(q, reads, writes, chain=False):
        toks = []
        for r in reads:
            toks += [wr[r]] if r in wr else []
            toks += [t for t in rd.get(r, []) if r[0] == "#" and t[0] != "c" + q]
        for w in writes:
            toks += rd.get(w, [])
            toks += [wr[w]] if w in wr and not (chain and wr[w][0] == "c" + q) else []
        most = {}
        for s, n in toks:
            most[s] = max(most.get(s, 0), n)
        for t in most.items():
            need(q, t)

    def mark(tok, reads, writes):
        for r in reads:
            rd.setdefault(r, []).append(tok)
        for w in writes:
            wr[w] = tok
            rd[w] = []

    def op(q, reads, writes, call, chain=False):
        order(q, reads, writes, chain)
        sem = "c" + q
        count[sem] += 1
        call().then_inc(T.sem[sem], 1)
        mark((sem, count[sem]), reads, writes)

    def dma(q, sem, total, out, in_, reads, writes):
        order(q, reads, writes)
        eng[q].dma_start(out, in_).then_inc(T.sem[sem], 16)
        mark((sem, total), reads, writes)

    off_chip = topo.engines(core, cores[direct[0]])
    on_chip = [e for e in topo.engines(core, relay[0][0]) if e not in off_chip]
    ne = len(off_chip)
    sent, stores, landed = [0], [0], {}

    def dst_id(c):
        rid, pid = topo.addr(c, core)
        return DstId(rid=rid, pnc=pid)

    def exchange(name, reads):
        kind, (a, b) = name[0], SENDS[name][3:]
        order("g", reads, [])

        def piece(q):
            lo = NB * a + other(q, rank) * (b - a)
            return T["snd" + kind][:, lo:lo + b - a]

        to = direct + [q for _, q in relay] * (name in DIRECT)
        d, h = ne // len(to), len(on_chip) // 4
        jobs = [(off_chip[i * d:(i + 1) * d], cores[q], "ar" + kind, piece(q), landing(T, name, rank, q)) for i, q in enumerate(to)]
        got = d * len(to)
        if name not in DIRECT:
            jobs += [(on_chip[lo * h:hi * h], c, "h" + name, piece(q), T["rel" + kind][:, a:b]) for (lo, hi), (c, q) in zip(share(name), relay)]
            got += ne * len(relay)
            if name in HAND:
                jobs = jobs[4:6] + [(off_chip,) + jobs[6][1:]] + jobs[:4]
            if name in FIVE:
                q = relay[2][1]
                jobs[-1] = (off_chip, cores[q], "ar" + kind, piece(q), landing(T, name, rank, q))
        while jobs:
            call, busy = [], []
            while jobs and not set(jobs[0][0]) & set(busy) and len(busy) < 2 * ne:
                es, c, sem, src, dst = jobs.pop(0)
                busy += es
                call.append(RemoteDMATransfer(dst_ids=[dst_id(c)], dma_engine_mask=bits(es), remote_sem=T.sem[sem], src=src, dst=dst))
            g.remote_dma_fused(call, local_sem=T.sem.sent)
            sent[0] += len(busy)
        landed[kind] = landed.get(kind, 0) + got
        wr["halo" + kind] = ("ar" + kind, landed[kind])

    def scaled(q, out, src, mul, add, read, res):
        if q == "s":
            op("s", [read], [res], lambda: S.activation(out, src, Act.Identity, bias=float(add), scale=float(mul)))
        else:
            op("v", [read], [res], lambda: V.tensor_scalar(out, src, float(mul), float(add), Op.mult, Op.add))

    def copy(q, out, src, reads, writes, chain=False):
        op(q, reads, writes, (lambda: V.tensor_copy(out, src)) if q == "v" else (lambda: S.activation(out, src, Act.Copy)), chain)

    def pick(q, src, out, reads, res):
        copy(q, out, src.indirect(T.shipU[:, 0:14]), reads + ["shipU"], [res])

    def ship(qs, win, snd, a, b, reads):
        n, lst = b - a, "ship%d" % (b - a)
        for i, q in enumerate(qs):
            lo, hi = 14 * n * i // len(qs) // 2 * 2, 14 * n * (i + 1) // len(qs) // 2 * 2
            copy(q, T[snd][:, a * R + 16 * lo:a * R + 16 * hi], T[win][:, OWN + a * R:OWN + b * R].indirect(T[lst][:, lo:hi]),
                 reads + [lst], ["%s%d%s" % (snd, a, q)])
        return ["%s%d%s" % (snd, a, q) for q in qs]

    op("v", [], ["colI"], lambda: V.memset(T.colI[:], 0))
    dma("q", "lship", 16, T.shipI[:], T.ship[:], [], ["shipI"])
    dma("s", "lspot", 16, T.spotI[:], T.spot[:], [], ["spotI"])
    order("q", ["colI"], [])
    order("s", ["colI"], [])
    for k in range(8):
        dma("sq"[k % 2], "lcol", 128, T.colI[16 * k:16 * k + 10, :], T.col[k, :], [], [])
    wr["colI"] = ("lcol", 128)
    dma("s", "lup", 16, T.A[:, OWN:WIN], T.val[:, 4 * R:10 * R], [], ["Aup"])
    dma("q", "ldg", 16, T.Dw[:, 0:R], T.val[:, 3 * R:4 * R], [], ["Dw"])
    dma("q", "llow", 16, T.lowd[:], T.val[:, 0:4 * R], [], ["lowd"])
    op("g", [], ["ioK"], lambda: g.iota(T.ioK[:], [[-1, 128]], 0, 1, allow_small_or_imprecise_dtypes=True))
    op("g", [], ["ioS"], lambda: g.iota(T.ioS[:], [[0, NB], [R, 6], [0, 2]], 0, 0, allow_small_or_imprecise_dtypes=True))
    op("g", [], ["ioJ"], lambda: g.iota(T.ioJ[:], [[-32, 5], [160, 2], [-1, 16]], -160, 1, allow_small_or_imprecise_dtypes=True))
    op("g", [], ["ioP"], lambda: g.iota(T.ioP[:], [[0, 1]], 0, 1))
    op("g", [], ["tab"], lambda: g.iota(T.tab[:], [[16, 14], [R, 3]], 0, 0, allow_small_or_imprecise_dtypes=True))
    diag = T.lowd[:, 3 * R:4 * R]

    def half(h, e):
        return slice(160 * h + 16 * (1 - e), 160 * h + 16 * (1 - e) + 128)

    def pair(out, a, b, alu, reads, res):
        op("v", reads, [res], lambda: V.tensor_tensor(out, a, b, alu), True)

    def init(bank, out, src, res, stop=False):
        op("p", [res, "idB"], [bank], lambda: P.matmul(out, T.idB[:], src, True, stop), True)

    def init_up(i):
        init("#B%d" % i, T["B%d" % i][:, 0:2 * R], T.A[:, OWN + 2 * i * R:OWN + (2 * i + 2) * R], "Aup")

    def start(v0):
        bank, n, z, res = group(v0)
        op("p", res + ["idN"], ["#" + bank], lambda: P.matmul(T[bank][:, 0:n], T.idN[:], T.Z[:, 0, z:z + n], True, False), True)

    def group(v0):
        lines, bank = GROUPS[v0]
        n = 42 * len(lines)
        z = 252 - n if 1 in lines else 0
        return bank, n, z, ["Z0", "Z1", "Z2"] + ["Z3"] * (n > 84) + ["Z4", "Z5"] * (z > 0)

    def prepare(word):
        c, q = word[:2], word[-1]
        n = int(word[1]) if word[1].isdigit() else None
        if c == "zz":
            for win in ("A", "U1", "U2"):
                op("v", [], [win + "z"], lambda: V.memset(T[win][:, 0:HALO], 0.0))
        elif c == "pm":
            op("v", ["ioP"], ["pmI"], lambda: V.tensor_scalar(T.pmI[:], T.ioP[:], 15, None, Op.bitwise_and))
        elif c == "pn":
            copy("v", T.pmF[:], T.pmI[:], ["pmI"], ["pmF"])
        elif c == "po":
            op("v", ["pmF", "tab"], ["tab"], lambda: V.tensor_scalar(T.tab[:], T.tab[:], T.pmF[:], None, Op.add))
        elif c == "Wf":
            scaled(q, T.Wf[:], T.W0[:], 1024, 0, "W", "Wf")
        elif c == "iP":
            scaled(q, T.idP[:], T.idB[:], R, 0, "idB", "idP")
            scaled(q, T.idM[:], T.idB[:], -R, 0, "idB", "idM")
        elif c == "KK":
            for h in range(2):
                for e in range(2):
                    op("p", ["Wf", "colT"], ["#XA0"], lambda: P.matmul(T.XA[:, 8:15, 3 * h:3 * h + 3], T.Wf[:, half(h, e)], T.colT[:, e:14:2, 0:3], e == 0, e == 1), True)
        elif c == "ka":
            for s in range(3):
                pair(T.key[:, :, 0, s], T.XA[:, 8:15, s:6:3], T.spotI[:, 14 * s:14 * s + 14], Op.add, ["#XA0", "spotI"], "key0")
        elif c == "kb":
            pair(T.key[:, :, 1, :], T.XA[:, 8:15, 0:6], T.tab[:], Op.add, ["#XA0", "tab"], "key1")
            copy("v", T.key[:, :, 2, :], T.XA[:, 8:15, 0:6], ["#XA0"], ["key2"])
        elif c == "o1":
            pair(T.tmp[:, 0, :, :], T.key[:, :, :, 0], T.key[:, :, :, 1], Op.min, ["key0", "key1", "key2"], "tmp0")
            pair(T.tmp[:, 1, :, :], T.key[:, :, :, 0], T.key[:, :, :, 1], Op.max, ["key0", "key1", "key2"], "tmp1")
        elif c == "o2":
            pair(T.tmp[:, 2, :, :], T.tmp[:, 0, :, :], T.key[:, :, :, 2], Op.max, ["tmp0"], "tmp2")
            pair(T.srt[:, 2, :, :], T.tmp[:, 0, :, :], T.key[:, :, :, 2], Op.min, ["tmp0"], "srt2")
        elif c == "o3":
            pair(T.srt[:, 0, :, :], T.tmp[:, 1, :, :], T.tmp[:, 2, :, :], Op.max, ["tmp1", "tmp2"], "srt0")
            pair(T.srt[:, 1, :, :], T.tmp[:, 1, :, :], T.tmp[:, 2, :, :], Op.min, ["tmp1", "tmp2"], "srt1")
        elif c == "ki":
            copy("v", T.srtI[:], T.srt[:, :, :, 0:2], ["srt0", "srt1", "srt2"], ["srtI"])
        elif c == "kl":
            op("v", ["srtI"], ["low"], lambda: V.tensor_scalar(T.low[:], T.srtI[:], 1023, None, Op.bitwise_and))
        elif c == "fU":
            copy("v", T.fromU[:], T.low[:, :, :, 1], ["low"], ["fromU"])
        elif c == "fG":
            copy("s", T.lowS[:], T.lowd[:, 0:3 * R].indirect(T.fromU[:, 0:42]), ["lowd", "fromU"], ["lowS"])
        elif c == "bk":
            for e in range(2):
                for h in range(2):
                    op("p", ["Wf", "srt0", "srt1"], ["#XA0"], lambda: P.matmul(T.XA[:, 16:18, e:14:2], T.Wf[:, half(e, h)], T.srt[:, 0:2, h:14:2, 2], h == 0, h == 1), True)
        elif c == "cm":
            pair(T.less[:, :, 0:2], T.key[:, :, 0, 0:2], T.key[:, :, 0, 1:3], Op.is_lt, ["key0"], "less")
            pair(T.less[:, :, 2], T.key[:, :, 0, 0], T.key[:, :, 0, 2], Op.is_lt, ["key0"], "less")
        elif c == "bP":
            for s, terms in enumerate(((("idM", 0), ("idM", 2)), (("idP", 0), ("idM", 1)), (("idP", 2), ("idP", 1)))):
                out = T.B0[:, 14 * s:14 * s + 14]
                op("p", ["tab", "idN"], ["#B0"], lambda: P.matmul(out, T.idN[:], T.tab[:, :, s], True, False), True)
                for i, (m, j) in enumerate(terms):
                    op("p", ["less", m], ["#B0"], lambda: P.matmul(out, T[m][:], T.less[:, :, j], False, i == 1), True)
        elif c == "bU":
            scaled("v", T.backU[:], T.B0[:, 0:42], -1, 0, "#B0", "backU")
        elif c == "B0":
            init_up(0)
        elif c == "iB":
            op("v", ["ioK"], ["idB"], lambda: V.tensor_scalar(T.idB[:], T.ioK[:], 0.0, None, Op.is_equal))
        elif c == "iN":
            op("v", ["ioK"], ["idN"], lambda: V.tensor_scalar(T.idN[:], T.ioK[:], 0.0, -1.0, Op.is_equal, Op.mult))
        elif c == "WW":
            for h in range(2):
                op("v", ["ioJ"], ["W"], lambda: V.tensor_scalar(T.W0[:, 160 * h:160 * h + 160], T.ioJ[:], float(16 * h), None, Op.is_equal), True)
        elif c[0] == "W":
            scaled(q, T.W[:, 320 * n:320 * n + 320], T.W0[:], LIFT + n, 0, "W", c)
        elif c == "sU":
            copy("v", T.shipU[:], T.shipI[:], ["shipI"], ["shipU"])
        elif c == "sB":
            copy("v", T.shipB[:], T.shipI[:], ["shipI"], ["shipB"])
            init("#XB0", T.XB[:, 0:NB, 0:12], T.ioS[:], "ioS")
            for w in range(6):
                op("p", ["shipB"], ["#XB0"], lambda: P.matmul(T.XB[:, 0:NB, 2 * w:2 * w + 2], T.idB[:], T.shipB[:], False, w == 5), True)
        elif c[0] == "s":
            copy("v", T["ship%d" % n][:], T.XB[:, 0:NB, 0:2 * n], ["#XB0"], ["ship%d" % n])
        elif c == "xC":
            pick("v", T.colI[:, 0:R], T.sndC[:], ["colI"], "sndC")
            exchange("C", ["sndC"])
        elif c == "cF":
            copy("v", T.colF[:, 0:R], T.colI[:], ["colI"], ["colF"])
        elif c == "cT":
            op("v", ["colF"], ["colT"], lambda: V.transpose(T.colT[:], T.colF[:, 0:R]))
        elif c[0] == "A":
            lo, hi = (0, ACUT) if q == "v" else (ACUT, 84)
            copy(q, T.sndA[:, 16 * lo:16 * hi], T.A[:, OWN:WIN].indirect(T.ship6[:, lo:hi]), ["Aup", "ship6"], ["snd" + c])
        elif c == "xA":
            exchange("A", ["sndAv", "sndAs"])
        elif c == "xD":
            pick("s", T.Dw[:, 0:R], T.sndD[:], ["Dw"], "sndD")
            exchange("D", ["sndD"])
        elif c == "pU":
            copy("v", T.spotU[:], T.low[:, :, :, 0], ["low"], ["spotU"])
        elif c == "hi":
            op("v", ["srtI"], ["hi"], lambda: V.tensor_scalar(T.hi[:], T.srtI[:, :, :, 0], 512 - H, None, Op.bitwise_and))
        elif c == "lg":
            op("v", ["hi"], ["lg"], lambda: V.tensor_scalar(T.lg[:], T.hi[:], float(R), None, Op.is_ge))
        elif c == "d2":
            scaled("v", T.d2[:], T.low[:, :, :, 0], 1.0 / R - 1.0 / H, 0.0, "low", "d2")
        elif c == "d1":
            scaled("v", T.d1[:], T.hi[:], -5.0 / H, (6 * R - HALO - 0.25) / H + (OWN + 0.25) / R, "hi", "d1")
        elif c == "nb":
            if q == "s":
                scaled("s", T.nbo[:], T.d2[:], 1.0 / 6, LIFT - (OWN + 0.25) / R, "d2", "nbo")
            else:
                scaled("v", T.nbo[:], T.low[:, :, :, 0], -1.0 / R, LIFT - (OWN + 0.25) / R, "low", "nbo")
        elif c == "t1":
            op("v", ["d1", "d2"], ["d1"], lambda: V.tensor_tensor(T.d1[:], T.d1[:], T.d2[:], Op.add))
        elif c == "td":
            scaled(q, T.Z[:, 1, 0:42], T.lg[:], H - R, R, "lg", "Z1")
        elif c == "t3":
            op("v", ["d1", "nbo"], ["Z0"], lambda: V.tensor_tensor(T.Z[:, 0, 0:42], T.d1[:], T.nbo[:], Op.add))
        elif c[0] == "Z":
            lo, a, b = ((42, 0, 42), (84, 0, 84), (168, 28, 42), (182, 14, 84))[n - 2]
            copy(q, T.Z[:, :, lo:lo + b - a], T.Z[:, :, a:b], ["Z0", "Z1"] + ["Z2"] * (b > 42), [c])
        elif c == "t2":
            op("v", ["d1", "lg"], ["d1"], lambda: V.tensor_tensor(T.d1[:], T.d1[:], T.lg[:], Op.mult))
        elif c == "r0":
            for w in range(6):
                copy("s", T.repU[:, 0:14, :, w], T.colT[:, :, 3:10], ["colT"], ["repU0"], True)
        elif c == "rL":
            for w in range(6):
                op("s", ["#XA0"], ["repL"], lambda: S.activation(T.repL[:, 14:42, w], T.XA[:, 16:18, 0:14], Act.Identity, scale=2.0 ** -20), True)
        elif c == "rM":
            copy("s", T.repL[:, 0:14, :], T.repL[:, 14:28, :], ["repL"], ["repM"])
        elif c == "rq":
            op("s", ["lowd"], ["rq0"], lambda: S.activation(T.rq[:, 0:R], diag, Act.Square, bias=2.0, scale=-1.0))
            op("s", ["lowd"], ["rr0"], lambda: S.activation(T.rr[:, 0:R], diag, Act.Identity, bias=4.0, scale=-2.0))
        elif c[0] == "r":
            out, src = T.repU[:, 14 * n:14 * n + 14, :, :], T.repU[:, 0:14, :, :]
            if q == "q":
                dma("q", "lrep%d" % n, 16, out, src, ["repU0"], ["repU%d" % n])
            else:
                copy(q, out, src, ["repU0"], ["repU%d" % n])
        elif c == "XA":
            init("#XA0", T.XA[:, 4:32, :], T.lowS[:, 0:2 * R], "lowS", True)
            init("#XA1", T.XA[:, 32:46, :], T.lowS[:, 2 * R:3 * R], "lowS", True)
        elif c == "go":
            start(n or int(q))
        elif c[0] == "g":
            copy(q, T.cug[:, n * R:(n + 1) * R], T.colF[:, 0:2 * R].indirect(T.spotU[:, 14 * n:14 * n + 14]),
                 ["colF", "haloC", "spotU"], ["cug%d" % n])
        else:
            op("v", ["cug%d" % n], ["#XB0", "#XB1"], lambda: V.transpose(T.XB[:, 14 * n:14 * n + 14, :], T.cug[:, n * R:(n + 1) * R]), n > 0)

    for word in PREPARE.split():
        prepare(word)

    def compare(v):
        lo, n, cut, rep, res = 252 * LINES.find(str(v)), 252, T.XB[:, 0:42, 4:10], T.repU[:, :, v - 2, :], ["repU0", "repU1", "repU2"]
        if v == 0:
            lo, n, cut, rep, res = 6 * 252, 84, T.XB[:, 28:42, 4:10], T.repL[:, 28:42, :], ["repL"]
        elif v == 1:
            lo, n, cut, rep, res = 6 * 252 + 84, 168, T.XB[:, 14:42, 4:10], T.repL[:, 0:28, :], ["repL", "repM"]
        op("v", ["#XB0", "#XB1"] + res, ["eq%d" % v], lambda: V.tensor_tensor(T.eq[:, lo:lo + n], cut, rep, Op.is_equal))

    def fold(v0):
        bank, n, z, _ = group(v0)
        lines, a = GROUPS[v0][0], 252 * LINES.find(str(v0))
        for h in range(2):
            for i in range(12):
                w, e = i // 2, i % 2
                lo = 320 * w + half(h, e).start
                op("p", ["eq%d" % v for v in lines + (0,) * (z > 0)] + ["W%d" % w], ["#" + bank],
                   lambda: P.matmul(T[bank][:, h:n:2], T.W[:, lo:lo + 128], T.eq[:, a + 6 * e + w:a + 6 * n:12], False, h == 1 and i == 11), True)

    def place(v0, step):
        bank, n, z, res = group(v0)
        a = 42 * LINES.find(str(v0))
        if step == 0:
            op("v", ["#" + bank] + res, ["jt%d" % v0], lambda: V.tensor_tensor(T.jt[:, a:a + n], T[bank][:, 0:n], T.Z[:, 1, z:z + n], Op.mult))
        else:
            copy("v", T.off[:, a:a + n], T.jt[:, a:a + n], ["jt%d" % v0], ["off%d" % v for v in GROUPS[v0][0]])

    def offsets(v, t, n):
        a = 42 * LINES.find(str(v)) + 14 * t
        return T.off[:, a:a + 14 * n]

    def sweep(k):
        win, new, snd = ("A", "U1", "U2")[k], ("U1", "U2", None)[k], ("snd1", "snd2", None)[k]
        whole = [win + "z", "halo" + "A12"[k]]  + (["Aup"] if k == 0 else [win + "u%d" % i for i in range(3)])
        xo, xn = ("XA", "XB", "XA")[k], ("XB", "XA", "XB")[k]
        x2, x2n = (T.lowS[:, 2 * R:3 * R], "lowS") if k < 2 else (T.x2[:], "x2")
        dg, words = T.J[:, 0:R], ORDER[k].split()
        third = [1] + [2] * ("d" not in words) + [3 + 2 * i + j for i in range(3) for j in range(2) if "g%d" % i in words]

        def gather(v, n):
            t = int(v == 1)
            op("s", whole + ["off%d" % v], ["G%d" % v] + ["P%d" % v] * (n - 2), lambda: S.activation(
                T.G[:, v, t * R:(t + n) * R], T[win][:, 0:WIN].indirect(offsets(v, t, n)), Act.Copy))

        def target(v, t):
            if v >= 3:
                i, j = (v - 3) // 2, (v - 3) % 2
                return "#B%d" % i, T["B%d" % i][:, j * R:(j + 1) * R]
            if v == 2:
                return "#J", dg
            s = int(t == 0)
            return "#%s0" % xn, T[xn][:, 4 + 14 * s:18 + 14 * s, :]

        def sub(v, t, res):
            bank, out = target(v, t)
            left[bank] -= 1
            op("p", [res, "idN"], [bank], lambda: P.matmul(out, T.idN[:], T.G[:, v, t * R:(t + 1) * R], False, left[bank] == 0), True)

        def fused(v):
            t = 2 * (v != 1)
            op("v", whole + ["off%d" % v, x2n], ["P%d" % v], lambda: V.tensor_tensor(
                T.G[:, v, t * R:(t + 1) * R], T[win][:, 0:WIN].indirect(offsets(v, t, 1)), x2, Op.mult))
            if v in third:
                sub(v, t, "P%d" % v)

        def times(v, n):
            t0 = int(v == 1)
            gv, res = T.G[:, v, t0 * R:(t0 + n) * R], ["G%d" % v] + ["P%d" % v] * (n - 2)
            op("v", res + ["#%s%d" % (xo, j) for j in range(t0 + n - 1)], res,
               lambda: V.tensor_tensor(gv, gv, T[xo][:, 4 + 14 * t0:4 + 14 * (t0 + n), :], Op.mult))
            for t in range(t0, t0 + (n if v in third else 2)):
                sub(v, t, res[0])

        def store(q, out, src, res):
            dma(q, "st", 0, out, src, res, [])
            stores[0] += 16

        def fin(i, j0, j1, q):
            lo, hi = (2 * i + j0) * R, (2 * i + j1) * R
            out = T[new][:, OWN + lo:OWN + hi] if new else T.Y[:, 4 * R + lo:4 * R + hi]
            res = (new + "u%d" % i) if new else "Y%d" % lo
            if 3 + 2 * i in third:
                copy("s", out, T["B%d" % i][:, j0 * R:j1 * R], ["#B%d" % i], [res])
            else:
                op("v", ["#B%d" % i] + ["P%d" % (3 + 2 * i + j) for j in range(j0, j1)], [res], lambda: V.tensor_tensor(
                    out, T["B%d" % i][:, j0 * R:j1 * R], T.G[:, 3 + 2 * i + j0:3 + 2 * i + j1, 2 * R:3 * R], Op.subtract))
            if not new:
                store(q, T.y[:, 4 * R + lo:4 * R + hi], out, [res])

        def init_low():
            init("#%s0" % xn, T[xn][:, 4:32, :], T.lowS[:, 0:2 * R], "lowS")
            init("#%s1" % xn, T[xn][:, 32:46, :], T.lowS[:, 2 * R:3 * R], "lowS", True)
            init("#J", dg, diag, "lowd")

        def diagonal():
            out, res = (dg, "#J") if k < 2 else (T.Y[:, 3 * R:4 * R], "Yd")
            op("v", ["#J", "P2"], [res], lambda: V.tensor_tensor(out, dg, T.G[:, 2, 2 * R:3 * R], Op.subtract))

        def newton(step):
            if step == 0:
                op("v", ["#J", "rq%d" % k], ["#J"], lambda: V.tensor_tensor(dg, dg, T.rq[:, k * R:(k + 1) * R], Op.mult))
                return
            out, res = (T.Rw[:, 0:R], "r2") if k == 0 else (T.r3[:], "r3")
            op("v", ["#J", "rr%d" % k], [res], lambda: V.tensor_tensor(out, T.rr[:, k * R:(k + 1) * R], dg, Op.subtract))
            if k == 1:
                store("q", T.inv[:], T.r3[:], ["r3"])

        def weigh():
            banks = ["#%s0" % xn, "#%s1" % xn]
            out, res = (T[xn][:, 4:46, :], banks) if k == 1 else (T.Ys[:], ["Ys"])
            op("v", banks + ["rg%d" % k], res, lambda: V.tensor_tensor(out, T[xn][:, 4:46, :], T.rg[:, (k - 1) * 3 * R:k * 3 * R], Op.mult))

        def r_round():
            pick("s", T.Rw[:, 0:R], T.sndR[:], ["r2"], "sndR")
            exchange("R", ["sndR"])

        left = {}
        for v in range(1, 9):
            for t in range(3 if v in third else 2):
                left[target(v, t)[0]] = left.get(target(v, t)[0], 0) + 1
        for word in words:
            c, a = word[0], word[1:]
            n = int(a) if a.isdigit() else None
            if c == ".":
                prepare(a)
            elif c in "GH":
                gather(n, 2 + (c == "H"))
            elif c in "MN":
                times(n, 2 + (c == "N"))
            elif c == "F":
                fused(n)
            elif c in "fg":
                fin(n, 0, 2, "q")
            elif c == "z":
                fin(2, n, n + 1, "qs"[n])
            elif c in "xX":
                lo, hi = CHUNKS[n]
                made = [new + "u%d" % i for i in range(lo // 2, hi // 2)]
                exchange("%d%d" % (k + 1, n), ship("s" if c == "x" else "sv", new, snd, lo, hi, made))
            elif word == "iL":
                init_low()
            elif c == "i":
                init_up(int(a[1]))
            elif c == "e":
                compare(n)
            elif c == "l":
                fold(n)
            elif c == "q":
                op("s", ["r2"], ["rq1"], lambda: S.activation(T.rq[:, R:2 * R], T.Rw[:, 0:R], Act.Square))
                op("s", ["r2"], ["rr1"], lambda: S.activation(T.rr[:, R:2 * R], T.Rw[:, 0:R], Act.Identity, scale=2.0))
            elif c in "ab":
                place(n, c == "b")
            elif c == "u":
                copy("s", T.Y[:, 0:3 * R], T.Ys[:, 0:3 * R].indirect(T.backU[:, 0:42]), ["Ys", "backU"], ["Yl"])
            elif word == "c2":
                copy("s", T.x2[:], T[xn][:, 32:46, :], ["#%s1" % xn], ["x2"])
            elif word == "c3":
                op("v", ["lowS", "rg1"], ["x2"], lambda: V.tensor_tensor(T.x2[:], T.lowS[:, 2 * R:3 * R], T.rg[:, 2 * R:3 * R], Op.mult))
            elif c == "d":
                diagonal()
            elif c == "D":
                copy("s", T.Y[:, 3 * R:4 * R], dg, ["#J"], ["Yd"])
            elif c == "n":
                newton(n)
            elif c == "w":
                weigh()
            elif c == "y":
                store("q", T.y[:, 0:4 * R], T.Y[:, 0:4 * R], ["Yl", "Yd"])
            elif word == "rA":
                op("s", ["Dw", "haloD", "spotU"], ["rg1"], lambda: S.activation(
                    T.rg[:, 0:3 * R], T.Dw[:, 0:2 * R].indirect(T.spotU[:, 0:42]), Act.Identity, bias=2.0, scale=-1.0))
            elif word == "rB":
                copy("s", T.rg[:, 3 * R:6 * R], T.Rw[:, 0:2 * R].indirect(T.spotU[:, 0:42]), ["r2", "haloR", "spotU"], ["rg2"])
            else:
                r_round()

    for k in range(3):
        sweep(k)
    for sem, n in count.items():
        need("g", (sem, n))
    need("g", ("sent", sent[0]))
    need("g", ("st", stores[0]))
